import numpy as np
import ml_dtypes


def mxq(x, axis, fmt="e4m3"):
    dtype, down = {"e4m3": (ml_dtypes.float8_e4m3fn, 7), "e5m2": (ml_dtypes.float8_e5m2, 14)}[fmt]
    v = np.moveaxis(np.asarray(x, np.float32).astype(ml_dtypes.bfloat16).astype(np.float64), axis, -1)
    blocks = v.reshape(v.shape[:-1] + (-1, 32))
    amax = np.abs(blocks).max(-1, keepdims=True)
    byte = np.maximum(np.where(amax > 0, np.frexp(amax)[1] - 1 + 127, 0) - down, 1)
    scale = np.exp2(byte - 127.0)
    codes = (blocks / scale).astype(np.float32).astype(dtype).astype(np.float64)
    return np.moveaxis((codes * scale).reshape(v.shape), -1, axis)


WIDE = False


def mx_kscale(k):
    if not WIDE:
        return np.ones(k)
    levels = np.array([10, -10, 5, -5, 0])
    if k % 512:
        return np.exp2(np.random.permutation(np.resize(levels, k // 32))).repeat(32)
    a = np.empty((k // 512, 16))
    for p in range(k // 512):
        a[p, :8] = np.random.permutation(np.resize(levels, 8))
        for g in range(8):
            far = levels[np.abs(levels - a[p, g]) >= 10]
            a[p, g + 8] = far[np.random.randint(len(far))]
    return np.exp2(a.ravel()).repeat(32)


def f64(x):
    return np.asarray(x).astype(np.float64)


def striped(idx):
    return np.tile(idx.reshape(-1, 16).T, (8, 1)).astype(np.uint16)


def unstriped(offs):
    return offs[:16].T.reshape(-1).astype(np.int64)


E2M1 = np.array([0.0, 0.5, 1.0, 1.5, 2.0, 3.0, 4.0, 6.0, -0.0, -0.5, -1.0, -1.5, -2.0, -3.0, -4.0, -6.0])


def pack_weight(w, fmt):
    k, n = w.shape
    w = f64(np.asarray(w, np.float32).astype(ml_dtypes.bfloat16)).reshape(k // 32, 32, n)
    amax = np.abs(w).max(1)
    if fmt == "e4m3":
        byte = np.frexp(amax)[1] - 1 + 127 - 7
    else:
        mant, ex = np.frexp(amax / 6.0)
        byte = np.where(mant > 0.5, ex, ex - 1) + 127
    byte = np.clip(np.where(amax > 0, byte, 1), 1, 254)
    scaled = (w * np.exp2(127.0 - byte)[:, None, :]).reshape(k, n).astype(np.float32)
    by_word = np.ascontiguousarray(scaled.reshape(k // 512, 128, 4, n).transpose(0, 1, 3, 2))
    if fmt == "e4m3":
        words = by_word.astype(ml_dtypes.float8_e4m3fn).view(np.uint8)
    else:
        c = by_word.astype(ml_dtypes.float4_e2m1fn).view(np.uint8) & 0xF
        words = (c[..., 0::2] | (c[..., 1::2] << 4)).reshape(k // 512, 128, 2 * n)
    return np.ascontiguousarray(words), np.ascontiguousarray(byte.astype(np.uint8).reshape(k // 512, 16, n))


def unpack_weight(words, scales, fmt):
    g, _, n = scales.shape
    words = np.ascontiguousarray(words).reshape(g, 128, n, -1)
    if fmt == "e4m3":
        vals = words.view(ml_dtypes.float8_e4m3fn).astype(np.float64)
    else:
        nib = np.empty((g, 128, n, 4), np.uint8)
        nib[..., 0::2] = words & 0xF
        nib[..., 1::2] = words >> 4
        vals = E2M1[nib]
    vals = vals * np.repeat(np.exp2(scales.astype(np.float64) - 127.0), 8, axis=1)[..., None]
    return vals.transpose(0, 1, 3, 2).reshape(g * 512, n)


def gelu(v):
    return 0.5 * v * (1.0 + np.tanh(np.sqrt(2.0 / np.pi) * (v + 0.044715 * v**3)))


def bf(x):
    return np.asarray(x, np.float32).astype(ml_dtypes.bfloat16)


def planes(Y):
    n, m = Y.shape
    b = f64(bf(Y)).reshape(n // 32, 32, m)
    amax = np.abs(b).max(1)
    byte = np.clip(np.where(amax > 0, np.frexp(amax)[1] - 1 + 127 - 7, 1), 1, 254)
    codes = (b * np.exp2(127.0 - byte)[:, None, :]).reshape(n, m).astype(np.float32).astype(ml_dtypes.float8_e4m3fn).view(np.uint8)
    words = codes.reshape(n // 512, 128, 4, m).transpose(0, 1, 3, 2)
    return np.ascontiguousarray(words), np.ascontiguousarray(byte.astype(np.uint8).reshape(n // 512, 16, m))


K, T, S, H, N, P = 1024, 4096, 1024, 1024, 512, 512

def setup_inputs():
    n = np.random.standard_normal
    s = mx_kscale(K)[:, None]
    u = mx_kscale(H)[:, None]
    e = np.exp(0.8 * n(N))
    d = {}
    d["tab_words"], d["tab_scales"] = pack_weight(n((K, T)) * s, "e4m3")
    d["offs"] = striped(np.random.permutation(T)[:S])
    d["pos1"] = striped(np.random.permutation(S)[:P])
    d["pos2"] = striped(np.random.permutation(S)[:P])
    d["w1"] = (0.55 * n((K, H)) / s / K ** 0.5).astype(np.float32)
    d["gain"] = (np.exp(0.3 * n(H)) * u[:, 0]).astype(np.float32)
    d["w2_words"], d["w2_scales"] = pack_weight(1.2 * n((H, N)) / u / H ** 0.5 * e, "e2m1")
    d["w3"] = (n((K, N)) / s / K ** 0.5 * e).astype(np.float32)
    d["base"] = (0.8 * n((N, P)) * e[:, None]).astype(np.float32)
    return d

def reference(tab_words, tab_scales, offs, pos1, pos2, w1, gain, w2_words, w2_scales, w3, base):
    v = unpack_weight(tab_words, tab_scales, "e4m3")[:, unstriped(offs)]
    w2 = unpack_weight(w2_words, w2_scales, "e2m1")
    f = mxq(f64(w1), 0, "e4m3").T @ v
    h = (f - np.cos(f)) * f64(gain)[:, None]
    skip = mxq(f64(w3), 0, "e4m3").T @ v
    g2 = (w2.T @ mxq(h, 0, "e4m3")) + np.abs(skip)
    y = np.maximum(g2[:, unstriped(pos1)], g2[:, unstriped(pos2)]) - f64(base)
    words, scales = planes(y)
    return y, words, scales

@@ -1,0 +1,307 @@
+import math
+from contextlib import ExitStack
+
+import concourse.mybir as mybir
+
+K, T, S, H, N, M = 1024, 4096, 1024, 1024, 512, 512
+FLOPS = 2 * K * H * S + 2 * K * N * S + 2 * H * N * S
+
+F32 = mybir.dt.float32
+BF16 = mybir.dt.bfloat16
+I32 = mybir.dt.int32
+U32 = mybir.dt.uint32
+U16 = mybir.dt.uint16
+U8 = mybir.dt.uint8
+E4M3 = mybir.dt.float8_e4m3fn_x4
+E2M1 = mybir.dt.float4_e2m1fn_x4
+ACT = mybir.ActivationFunctionType
+ALU = mybir.AluOpType
+
+P = 128
+HALF = 512
+CH = 128
+
+
+def tile_list_scaffold_lashing_features_kernel(
+    tc, tab_words, tab_scales, offs, pos1, pos2, w1, gain, w2_words, w2_scales, w3, base, out_0, out_1, out_2
+):
+    nc = tc.nc
+    with ExitStack() as ctx:
+        keep = ctx.enter_context(tc.tile_pool(name="keep", bufs=1))
+        ring = ctx.enter_context(tc.tile_pool(name="ring", bufs=4))
+        stage = ctx.enter_context(tc.tile_pool(name="stage", bufs=3))
+        tail = ctx.enter_context(tc.tile_pool(name="tail", bufs=2))
+        psum = ctx.enter_context(tc.psum_pool(name="psum", bufs=8))
+
+        def kept(shape, dtype, name):
+            return keep.tile(shape, dtype, name=name, align_bytes=64)
+
+        offs_t = keep.tile([P, S // 16], U16, name="offs_t")
+        pos1_t = keep.tile([P, M // 16], U16, name="pos1_t")
+        pos2_t = keep.tile([P, M // 16], U16, name="pos2_t")
+
+        tabw = [kept([P, T], I32, f"tabw{a}") for a in range(2)]
+        tabs = kept([P, T], U8, "tabs")
+        w2w_raw = kept([P, 2, 2 * N], U8, "w2w_raw")
+        w2s_raw = kept([P, 2, N], U8, "w2s_raw")
+        gain_t = kept([P, 2, 4], F32, "gain_t")
+        base_t = kept([P, 4, M], F32, "base_t")
+        raw = {}
+        for name in ("w10", "w11", "w3"):
+            for a in range(2):
+                raw[name, a] = kept([P, 4, HALF], F32, f"raw_{name}_{a}")
+
+        def weight_rows(name, a):
+            rows = slice(HALF * a, HALF * (a + 1))
+            if name == "w3":
+                src = w3[rows, :]
+            else:
+                b = 0 if name == "w10" else 1
+                src = w1[rows, HALF * b : HALF * (b + 1)]
+            return src.rearrange("(p j) c -> p j c", j=4)
+
+        nc.vector.memset(tabs[:].bitcast(I32), 0)
+        nc.gpsimd.memset(w2s_raw[:].rearrange("p a c -> p (a c)").bitcast(I32), 0)
+
+        nc.sync.dma_start(offs_t[:], offs)
+        nc.sync.dma_start(pos1_t[:], pos1)
+        nc.sync.dma_start(pos2_t[:], pos2)
+        nc.sync.dma_start(gain_t[:], gain.rearrange("(b p t) -> p b t", b=2, t=4))
+        nc.sync.dma_start(w2w_raw[:].bitcast(I32), w2_words.rearrange("a p c -> p a c").bitcast(I32))
+        for a in range(2):
+            nc.sync.dma_start(raw["w10", a][:], weight_rows("w10", a))
+        for a in range(2):
+            nc.sync.dma_start(tabw[a][:], tab_words[a].rearrange("p t i -> p (t i)").bitcast(I32))
+            if a == 0:
+                for q in range(4):
+                    nc.sync.dma_start(
+                        tabs[32 * q : 32 * q + 8, :].bitcast(I32), tab_scales[:, 4 * q : 4 * q + 4, :].bitcast(I32)
+                    )
+        for name in ("w11", "w3"):
+            for a in range(2):
+                nc.sync.dma_start(raw[name, a][:], weight_rows(name, a))
+        nc.sync.dma_start(base_t[:], base.rearrange("(p t) m -> p t m", t=4))
+
+        for q in range(4):
+            nc.gpsimd.dma_start(
+                w2s_raw[32 * q : 32 * q + 4, :, :].bitcast(I32),
+                w2_scales[:, 4 * q : 4 * q + 4, :].rearrange("a r c -> r a c").bitcast(I32),
+            )
+
+        grouped = {}
+        wq = {}
+        ws = {}
+
+        def cast_weight(name, a, eng):
+            grouped[name, a] = stage.tile([P, 4, P, 4], BF16, name="grp", align_bytes=64)
+            dst = grouped[name, a][:].rearrange("p t m j -> p m j t")
+            src = raw[name, a][:].rearrange("p j (m t) -> p m j t", t=4)
+            if eng == "S":
+                nc.scalar.copy(dst, src)
+            else:
+                nc.vector.tensor_copy(dst, src)
+
+        def quant_weight(name, a):
+            wq[name, a] = kept([P, HALF], U32, f"wq_{name}_{a}")
+            ws[name, a] = kept([P, HALF], U8, f"ws_{name}_{a}")
+            nc.vector.quantize_mx(
+                out=wq[name, a][:].bitcast(E4M3),
+                scales=ws[name, a][:],
+                in_=grouped[name, a][:].rearrange("p t m j -> p (t m j)"),
+            )
+
+        w2w = kept([P, 2, 4, P, 2], U8, "w2w")
+        w2s = kept([P, 2, 4, P], U8, "w2s")
+        for a in range(2):
+            nc.vector.tensor_copy(
+                w2w[:, a].rearrange("p t q e -> p q t e"), w2w_raw[:, a, :].rearrange("p (q t e) -> p q t e", t=4, e=2)
+            )
+        nc.vector.tensor_copy(
+            w2s[:].rearrange("p a t q -> p a q t"), w2s_raw[:].rearrange("p a (q t) -> p a q t", t=4)
+        )
+
+        for a in range(2):
+            cast_weight("w10", a, "S")
+            quant_weight("w10", a)
+
+        vs = kept([P, S], U8, "vs")
+        nc.vector.tensor_copy(vs[:], tabs[:].indirect(offs_t[:]))
+        vw = {}
+
+        def gather_words(a, hf):
+            vw[a, hf] = kept([P, HALF], U32, f"vw{a}{hf}")
+            nc.vector.tensor_copy(vw[a, hf][:], tabw[a][:].bitcast(U32).indirect(offs_t[:, 32 * hf : 32 * (hf + 1)]))
+
+        gather_words(0, 0)
+        gather_words(0, 1)
+        gather_words(1, 0)
+
+        hq = {}
+        hs = {}
+        for b in range(2):
+            for hf in range(2):
+                hq[b, hf] = kept([P, HALF], U32, f"hq{b}{hf}")
+                hs[b, hf] = kept([P, HALF], U8, f"hs{b}{hf}")
+
+        units = [(b, c) for b in range(2) for c in range(S // CH)]
+        diff = {}
+        hb = {}
+
+        def first_half(u):
+            b, c = units[u]
+            hf, c0 = divmod(c * CH, HALF)
+            name = "w10" if b == 0 else "w11"
+            bank = psum.tile([P, 4, CH], F32, name="bank", tag="bank")
+            for t in range(4):
+                for a in range(2):
+                    nc.tensor.matmul_mx(
+                        out=bank[:, t, :],
+                        lhsT=wq[name, a][:, P * t : P * (t + 1)].bitcast(E4M3),
+                        lhsT_scale=ws[name, a][:, P * t : P * (t + 1)],
+                        rhs=vw[a, hf][:, c0 : c0 + CH].bitcast(E4M3),
+                        rhs_scale=vs[4 * a : P, c * CH : (c + 1) * CH],
+                        start=(a == 0),
+                        stop=(a == 1),
+                    )
+            woven = bank[:].rearrange("p t n -> p n t")
+            sine = ring.tile([P, CH, 4], F32, name="sine")
+            nc.scalar.activation(sine[:], woven, ACT.Sin, scale=0.5)
+            versine = ring.tile([P, CH, 4], F32, name="versine")
+            nc.scalar.activation(versine[:], sine[:], ACT.Square, scale=math.sqrt(2.0))
+            diff[u] = ring.tile([P, CH, 4], F32, name="diff")
+            nc.vector.scalar_tensor_tensor(diff[u][:], woven, -1.0, versine[:], ALU.add, ALU.add)
+
+        def apply_gain(u):
+            b, c = units[u]
+            hb[u] = ring.tile([P, CH, 4], BF16, name="hb", align_bytes=64)
+            nc.vector.tensor_tensor(hb[u][:], diff[u][:], gain_t[:, b : b + 1, :].to_broadcast([P, CH, 4]), ALU.mult)
+
+        def quant_h(u):
+            b, c = units[u]
+            hf, c0 = divmod(c * CH, HALF)
+            nc.vector.quantize_mx(
+                out=hq[b, hf][:, c0 : c0 + CH].bitcast(E4M3),
+                scales=hs[b, hf][:, c0 : c0 + CH],
+                in_=hb[u][:].rearrange("p n t -> p (n t)"),
+            )
+
+        g2 = [kept([P, S], F32, f"g2_{t}") for t in range(4)]
+
+        def skip_part(t, hf):
+            bank = psum.tile([P, HALF], F32, name="bank", tag="bank")
+            for a in range(2):
+                nc.tensor.matmul_mx(
+                    out=bank[:],
+                    lhsT=wq["w3", a][:, P * t : P * (t + 1)].bitcast(E4M3),
+                    lhsT_scale=ws["w3", a][:, P * t : P * (t + 1)],
+                    rhs=vw[a, hf][:].bitcast(E4M3),
+                    rhs_scale=vs[4 * a : P, HALF * hf : HALF * (hf + 1)],
+                    start=(a == 0),
+                    stop=(a == 1),
+                )
+            nc.scalar.activation(g2[t][:, HALF * hf : HALF * (hf + 1)], bank[:], ACT.Abs)
+
+        def second_part(t, hf):
+            bank = psum.tile([P, HALF], F32, name="bank", tag="bank")
+            for b in range(2):
+                nc.tensor.matmul_mx(
+                    out=bank[:],
+                    lhsT=w2w[:, b, t].rearrange("p q e -> p (q e)").bitcast(E2M1),
+                    lhsT_scale=w2s[:, b, t, :],
+                    rhs=hq[b, hf][:].bitcast(E4M3),
+                    rhs_scale=hs[b, hf][:],
+                    start=(b == 0),
+                    stop=(b == 1),
+                )
+            cols = slice(HALF * hf, HALF * (hf + 1))
+            nc.vector.tensor_tensor(g2[t][:, cols], bank[:], g2[t][:, cols], ALU.add)
+
+        last = len(units) - 1
+        for u in range(len(units) + 2):
+            if u <= last:
+                first_half(u)
+            if 1 <= u <= last + 1:
+                apply_gain(u - 1)
+            if u >= 2:
+                quant_h(u - 2)
+            if u == 0:
+                gather_words(1, 1)
+            if u in (3, 5):
+                cast_weight("w11", (u - 3) // 2, "S")
+            if u in (4, 6):
+                quant_weight("w11", (u - 4) // 2)
+            if u in (8, 9):
+                cast_weight("w3", u - 8, "V")
+            if u in (9, 10):
+                quant_weight("w3", u - 9)
+            if 11 <= u <= 14:
+                skip_part(u - 11, 0)
+            if u == 15:
+                skip_part(0, 1)
+            if u >= 16:
+                second_part(u - 16, 0)
+
+        y = kept([P, 4, M], F32, "y")
+        out0_v = out_0.rearrange("(p t) m -> p t m", t=4)
+
+        def pair(t, m0, m1):
+            w = m1 - m0
+            left = tail.tile([P, w], F32, name="left")
+            right = tail.tile([P, w], F32, name="right")
+            larger = tail.tile([P, w], F32, name="larger")
+            nc.vector.tensor_copy(left[:], g2[t][:].indirect(pos1_t[:, m0 // 16 : m1 // 16]))
+            nc.vector.tensor_copy(right[:], g2[t][:].indirect(pos2_t[:, m0 // 16 : m1 // 16]))
+            return left, right, larger
+
+        def finish(t, m0, m1, left, right, larger):
+            nc.vector.tensor_tensor(larger[:], left[:], right[:], ALU.max)
+
+        def subtract(t, m0, m1, larger):
+            nc.vector.tensor_tensor(y[:, t, m0:m1], larger[:], base_t[:, t, m0:m1], ALU.subtract)
+            nc.sync.dma_start(out0_v[:, t, m0:m1], y[:, t, m0:m1])
+
+        yq = kept([P, M], U32, "yq")
+        ys = kept([P, M], U8, "ys")
+        yb = {}
+
+        def cast_y(m0, m1, eng):
+            yb[m0] = kept([P, m1 - m0, 4], BF16, f"yb{m0}")
+            dst = yb[m0][:].rearrange("p (c i) t -> p c t i", i=4)
+            src = y[:, :, m0:m1].rearrange("p t (c i) -> p c t i", i=4)
+            if eng == "S":
+                nc.scalar.copy(dst, src)
+            else:
+                nc.vector.tensor_copy(dst, src)
+
+        def quant_y(m0, m1):
+            nc.vector.quantize_mx(
+                out=yq[:, m0:m1].bitcast(E4M3), scales=ys[:, m0:m1], in_=yb[m0][:].rearrange("p m t -> p (m t)")
+            )
+            nc.scalar.dma_start(
+                out_1[0].rearrange("p m t -> p (m t)").bitcast(I32)[:, m0:m1], yq[:, m0:m1].bitcast(I32)
+            )
+
+        second_part(0, 1)
+        second_part(2, 0)
+        second_part(3, 0)
+        pieces = [(0, 0, M), (1, 0, M), (2, 0, M), (3, 0, M // 2), (3, M // 2, M)]
+        held = None
+        for t, m0, m1 in pieces:
+            if t < 3:
+                skip_part(t + 1, 1)
+            tiles = pair(t, m0, m1)
+            if held is not None:
+                subtract(*held)
+            if t < 3:
+                second_part(t + 1, 1)
+            finish(t, m0, m1, *tiles)
+            held = (t, m0, m1, tiles[2])
+            if (t, m0) == (3, M // 2):
+                cast_y(0, M // 2, "S")
+        subtract(*held)
+        quant_y(0, M // 2)
+        cast_y(M // 2, M, "V")
+        quant_y(M // 2, M)
+        for q in range(4):
+            eng = nc.sync if q % 2 == 0 else nc.scalar
+            eng.dma_start(out_2[0, 4 * q : 4 * q + 4, :].bitcast(I32), ys[32 * q : 32 * q + 4, :].bitcast(I32))

@@ -2,6 +2,7 @@ import math
 from contextlib import ExitStack
 
 import concourse.mybir as mybir
+from concourse.masks import make_identity
 
 K, T, S, H, N, M = 1024, 4096, 1024, 1024, 512, 512
 FLOPS = 2 * K * H * S + 2 * K * N * S + 2 * H * N * S
@@ -20,6 +21,13 @@ ALU = mybir.AluOpType
 P = 128
 HALF = 512
 CH = 128
+GAIN = "GVGVGVGVGVGVGVGV"
+CASTS = {("w11", 0): (0, "VV"), ("w11", 1): (3, "SV"), ("w3", 0): (7, "SV"), ("w3", 1): (9, "SV")}
+SKIPS = {12: [(0, 0)], 13: [(1, 0)], 15: [(0, 1)]}
+SECONDS = {15: [(0, 0)], 16: [(1, 0)], 17: [(0, 1)]}
+TAIL_SKIPS = {0: [(1, 1), (2, 0)], 1: [(2, 1), (3, 0)], 2: [(3, 1)]}
+TAIL_SECONDS = {0: [(1, 1, "V"), (2, 0, "G")], 1: [(2, 1, "V"), (3, 0, "G")], 2: [(3, 1, "V")]}
+SUB = "GGGGV"
 
 
 def tile_list_scaffold_lashing_features_kernel(
@@ -31,7 +39,8 @@ def tile_list_scaffold_lashing_features_kernel(
         ring = ctx.enter_context(tc.tile_pool(name="ring", bufs=4))
         stage = ctx.enter_context(tc.tile_pool(name="stage", bufs=3))
         tail = ctx.enter_context(tc.tile_pool(name="tail", bufs=2))
-        psum = ctx.enter_context(tc.psum_pool(name="psum", bufs=8))
+        psum = ctx.enter_context(tc.psum_pool(name="psum", bufs=7))
+        psum_keep = ctx.enter_context(tc.psum_pool(name="psum_keep", bufs=1))
 
         def kept(shape, dtype, name):
             return keep.tile(shape, dtype, name=name, align_bytes=64)
@@ -42,14 +51,16 @@ def tile_list_scaffold_lashing_features_kernel(
 
         tabw = [kept([P, T], I32, f"tabw{a}") for a in range(2)]
         tabs = kept([P, T], U8, "tabs")
-        w2w_raw = kept([P, 2, 2 * N], U8, "w2w_raw")
+        w2w_raw = [kept([P, 2 * N], U8, f"w2w_raw{a}") for a in range(2)]
+        late = [kept([P, 4, 256], F32, f"late{e}") for e in range(2)]
         w2s_raw = kept([P, 2, N], U8, "w2s_raw")
         gain_t = kept([P, 2, 4], F32, "gain_t")
         base_t = kept([P, 4, M], F32, "base_t")
         raw = {}
         for name in ("w10", "w11", "w3"):
             for a in range(2):
-                raw[name, a] = kept([P, 4, HALF], F32, f"raw_{name}_{a}")
+                if (name, a) != ("w10", 1):
+                    raw[name, a] = kept([P, 4, HALF], F32, f"raw_{name}_{a}")
 
         def weight_rows(name, a):
             rows = slice(HALF * a, HALF * (a + 1))
@@ -60,6 +71,9 @@ def tile_list_scaffold_lashing_features_kernel(
                 src = w1[rows, HALF * b : HALF * (b + 1)]
             return src.rearrange("(p j) c -> p j c", j=4)
 
+        warm = keep.tile([P, 2], F32, name="warm")
+        nc.gpsimd.memset(warm[:, 0:1], 0.0)
+        nc.scalar.activation(warm[:, 1:2], warm[:, 0:1], ACT.Sin)
         nc.vector.memset(tabs[:].bitcast(I32), 0)
         nc.gpsimd.memset(w2s_raw[:].rearrange("p a c -> p (a c)").bitcast(I32), 0)
 
@@ -67,39 +81,49 @@ def tile_list_scaffold_lashing_features_kernel(
         nc.sync.dma_start(pos1_t[:], pos1)
         nc.sync.dma_start(pos2_t[:], pos2)
         nc.sync.dma_start(gain_t[:], gain.rearrange("(b p t) -> p b t", b=2, t=4))
-        nc.sync.dma_start(w2w_raw[:].bitcast(I32), w2_words.rearrange("a p c -> p a c").bitcast(I32))
         for a in range(2):
-            nc.sync.dma_start(raw["w10", a][:], weight_rows("w10", a))
-        for a in range(2):
-            nc.sync.dma_start(tabw[a][:], tab_words[a].rearrange("p t i -> p (t i)").bitcast(I32))
-            if a == 0:
-                for q in range(4):
-                    nc.sync.dma_start(
-                        tabs[32 * q : 32 * q + 8, :].bitcast(I32), tab_scales[:, 4 * q : 4 * q + 4, :].bitcast(I32)
-                    )
+            nc.sync.dma_start(w2w_raw[a][:].bitcast(I32), w2_words[a].bitcast(I32))
+        words = [tab_words[a].rearrange("p t i -> p (t i)").bitcast(I32) for a in range(2)]
+        for c0 in (0, T // 2):
+            nc.sync.dma_start(tabw[0][:, c0 : c0 + T // 2], words[0][:, c0 : c0 + T // 2])
+        for q in range(4):
+            nc.sync.dma_start(
+                tabs[32 * q : 32 * q + 8, :].bitcast(I32), tab_scales[:, 4 * q : 4 * q + 4, :].bitcast(I32)
+            )
+        nc.sync.dma_start(tabw[1][:], words[1])
+        for q in range(4):
+            nc.sync.dma_start(
+                w2s_raw[32 * q : 32 * q + 4, :, :].bitcast(I32),
+                w2_scales[:, 4 * q : 4 * q + 4, :].rearrange("a r c -> r a c").bitcast(I32),
+            )
+        nc.sync.dma_start(raw["w10", 0][:], weight_rows("w10", 0))
+        for e in range(2):
+            nc.sync.dma_start(late[e][:], weight_rows("w10", 1)[:, :, 256 * e : 256 * (e + 1)])
         for name in ("w11", "w3"):
             for a in range(2):
                 nc.sync.dma_start(raw[name, a][:], weight_rows(name, a))
         nc.sync.dma_start(base_t[:], base.rearrange("(p t) m -> p t m", t=4))
 
-        for q in range(4):
-            nc.gpsimd.dma_start(
-                w2s_raw[32 * q : 32 * q + 4, :, :].bitcast(I32),
-                w2_scales[:, 4 * q : 4 * q + 4, :].rearrange("a r c -> r a c").bitcast(I32),
-            )
-
         grouped = {}
         wq = {}
         ws = {}
 
-        def cast_weight(name, a, eng):
-            grouped[name, a] = stage.tile([P, 4, P, 4], BF16, name="grp", align_bytes=64)
-            dst = grouped[name, a][:].rearrange("p t m j -> p m j t")
-            src = raw[name, a][:].rearrange("p j (m t) -> p m j t", t=4)
+        def cast_columns(name, a, src, m0, m1, eng):
+            if (name, a) not in grouped:
+                grouped[name, a] = stage.tile([P, 4, P, 4], BF16, name="grp", align_bytes=64)
+            dst = grouped[name, a][:, :, m0:m1, :].rearrange("p t m j -> p m j t")
+            src = src.rearrange("p j (m t) -> p m j t", t=4)
             if eng == "S":
                 nc.scalar.copy(dst, src)
-            else:
+            elif eng == "V":
                 nc.vector.tensor_copy(dst, src)
+            else:
+                nc.gpsimd.tensor_scalar(dst, src, 1.0, 0.0, ALU.mult, ALU.add)
+
+        def cast_weight(name, a, engs):
+            w = P // len(engs)
+            for e, eng in enumerate(engs):
+                cast_columns(name, a, raw[name, a][:, :, 4 * w * e : 4 * w * (e + 1)], w * e, w * (e + 1), eng)
 
         def quant_weight(name, a):
             wq[name, a] = kept([P, HALF], U32, f"wq_{name}_{a}")
@@ -114,18 +138,22 @@ def tile_list_scaffold_lashing_features_kernel(
         w2s = kept([P, 2, 4, P], U8, "w2s")
         for a in range(2):
             nc.vector.tensor_copy(
-                w2w[:, a].rearrange("p t q e -> p q t e"), w2w_raw[:, a, :].rearrange("p (q t e) -> p q t e", t=4, e=2)
+                w2w[:, a].rearrange("p t q e -> p q t e"), w2w_raw[a][:].rearrange("p (q t e) -> p q t e", t=4, e=2)
             )
-        nc.vector.tensor_copy(
-            w2s[:].rearrange("p a t q -> p a q t"), w2s_raw[:].rearrange("p a (q t) -> p a q t", t=4)
-        )
 
-        for a in range(2):
-            cast_weight("w10", a, "S")
-            quant_weight("w10", a)
-
+        gain_w = kept([P, 2, CH, 4], F32, "gain_w")
+        nc.vector.tensor_copy(gain_w[:], gain_t[:].unsqueeze(2).to_broadcast([P, 2, CH, 4]))
+        ident = kept([P, P], F32, "ident")
+        make_identity(nc, ident[:])
+        turned = psum.tile([P, 2, P], F32, name="bank", tag="bank")
+        for b in range(2):
+            nc.tensor.transpose(turned[:, b, :], gain_w[:, b, 0:32, :].rearrange("p n t -> p (n t)"), ident[:])
+        gain_rows = kept([P, 2, P], F32, "gain_rows")
+        nc.scalar.copy(gain_rows[:], turned[:])
+        gain_bank = psum_keep.tile([P, 2, P], F32, name="gain_bank")
+        for b in range(2):
+            nc.tensor.transpose(gain_bank[:, b, :], gain_rows[:, b, :], ident[:])
         vs = kept([P, S], U8, "vs")
-        nc.vector.tensor_copy(vs[:], tabs[:].indirect(offs_t[:]))
         vw = {}
 
         def gather_words(a, hf):
@@ -134,7 +162,18 @@ def tile_list_scaffold_lashing_features_kernel(
 
         gather_words(0, 0)
         gather_words(0, 1)
+        nc.vector.tensor_copy(vs[:], tabs[:].indirect(offs_t[:]))
         gather_words(1, 0)
+        gather_words(1, 1)
+        cast_weight("w10", 0, "S")
+        quant_weight("w10", 0)
+        cast_columns("w10", 1, late[0][:], 0, 64, "V")
+        cast_columns("w10", 1, late[1][:, :, 0:160], 64, 104, "V")
+        cast_columns("w10", 1, late[1][:, :, 160:256], 104, 128, "S")
+        quant_weight("w10", 1)
+        nc.vector.tensor_copy(
+            w2s[:].rearrange("p a t q -> p a q t"), w2s_raw[:].rearrange("p a (q t) -> p a q t", t=4)
+        )
 
         hq = {}
         hs = {}
@@ -173,16 +212,25 @@ def tile_list_scaffold_lashing_features_kernel(
 
         def apply_gain(u):
             b, c = units[u]
-            hb[u] = ring.tile([P, CH, 4], BF16, name="hb", align_bytes=64)
-            nc.vector.tensor_tensor(hb[u][:], diff[u][:], gain_t[:, b : b + 1, :].to_broadcast([P, CH, 4]), ALU.mult)
+            if u % 2 == 0:
+                hb[u // 2] = ring.tile([P, 2, CH, 4], BF16, name="hb", align_bytes=64)
+            if GAIN[u] == "G":
+                nc.gpsimd.tensor_tensor(hb[u // 2][:, u % 2], diff[u][:], gain_w[:, b], ALU.mult)
+            else:
+                nc.vector.tensor_tensor(
+                    hb[u // 2][:, u % 2].rearrange("p (r n) t -> p r (n t)", r=4),
+                    diff[u][:].rearrange("p (r n) t -> p r (n t)", r=4),
+                    gain_bank[:, b : b + 1, :].to_broadcast([P, 4, P]),
+                    ALU.mult,
+                )
 
         def quant_h(u):
             b, c = units[u]
             hf, c0 = divmod(c * CH, HALF)
             nc.vector.quantize_mx(
-                out=hq[b, hf][:, c0 : c0 + CH].bitcast(E4M3),
-                scales=hs[b, hf][:, c0 : c0 + CH],
-                in_=hb[u][:].rearrange("p n t -> p (n t)"),
+                out=hq[b, hf][:, c0 : c0 + 2 * CH].bitcast(E4M3),
+                scales=hs[b, hf][:, c0 : c0 + 2 * CH],
+                in_=hb[u // 2][:].rearrange("p e n t -> p (e n t)"),
             )
 
         g2 = [kept([P, S], F32, f"g2_{t}") for t in range(4)]
@@ -201,7 +249,7 @@ def tile_list_scaffold_lashing_features_kernel(
                 )
             nc.scalar.activation(g2[t][:, HALF * hf : HALF * (hf + 1)], bank[:], ACT.Abs)
 
-        def second_part(t, hf):
+        def second_part(t, hf, on="V"):
             bank = psum.tile([P, HALF], F32, name="bank", tag="bank")
             for b in range(2):
                 nc.tensor.matmul_mx(
@@ -214,7 +262,12 @@ def tile_list_scaffold_lashing_features_kernel(
                     stop=(b == 1),
                 )
             cols = slice(HALF * hf, HALF * (hf + 1))
-            nc.vector.tensor_tensor(g2[t][:, cols], bank[:], g2[t][:, cols], ALU.add)
+            if on == "V":
+                nc.vector.tensor_tensor(g2[t][:, cols], bank[:], g2[t][:, cols], ALU.add)
+            else:
+                part = tail.tile([P, HALF], F32, name="part")
+                nc.scalar.copy(part[:], bank[:])
+                nc.gpsimd.tensor_tensor(g2[t][:, cols], part[:], g2[t][:, cols], ALU.add)
 
         last = len(units) - 1
         for u in range(len(units) + 2):
@@ -222,24 +275,17 @@ def tile_list_scaffold_lashing_features_kernel(
                 first_half(u)
             if 1 <= u <= last + 1:
                 apply_gain(u - 1)
-            if u >= 2:
-                quant_h(u - 2)
-            if u == 0:
-                gather_words(1, 1)
-            if u in (3, 5):
-                cast_weight("w11", (u - 3) // 2, "S")
-            if u in (4, 6):
-                quant_weight("w11", (u - 4) // 2)
-            if u in (8, 9):
-                cast_weight("w3", u - 8, "V")
-            if u in (9, 10):
-                quant_weight("w3", u - 9)
-            if 11 <= u <= 14:
-                skip_part(u - 11, 0)
-            if u == 15:
-                skip_part(0, 1)
-            if u >= 16:
-                second_part(u - 16, 0)
+            if u >= 3 and u % 2 == 1:
+                quant_h(u - 3)
+            for (name, a), (when, engs) in CASTS.items():
+                if u == when:
+                    cast_weight(name, a, engs)
+                if u == when + 1:
+                    quant_weight(name, a)
+            for t, hf in SKIPS.get(u, ()):
+                skip_part(t, hf)
+            for t, hf in SECONDS.get(u, ()):
+                second_part(t, hf)
 
         y = kept([P, 4, M], F32, "y")
         out0_v = out_0.rearrange("(p t) m -> p t m", t=4)
@@ -256,8 +302,9 @@ def tile_list_scaffold_lashing_features_kernel(
         def finish(t, m0, m1, left, right, larger):
             nc.vector.tensor_tensor(larger[:], left[:], right[:], ALU.max)
 
-        def subtract(t, m0, m1, larger):
-            nc.vector.tensor_tensor(y[:, t, m0:m1], larger[:], base_t[:, t, m0:m1], ALU.subtract)
+        def subtract(t, m0, m1, larger, on):
+            eng = nc.vector if on == "V" else nc.gpsimd
+            eng.tensor_tensor(y[:, t, m0:m1], larger[:], base_t[:, t, m0:m1], ALU.subtract)
             nc.sync.dma_start(out0_v[:, t, m0:m1], y[:, t, m0:m1])
 
         yq = kept([P, M], U32, "yq")
@@ -281,21 +328,18 @@ def tile_list_scaffold_lashing_features_kernel(
                 out_1[0].rearrange("p m t -> p (m t)").bitcast(I32)[:, m0:m1], yq[:, m0:m1].bitcast(I32)
             )
 
-        second_part(0, 1)
-        second_part(2, 0)
-        second_part(3, 0)
         pieces = [(0, 0, M), (1, 0, M), (2, 0, M), (3, 0, M // 2), (3, M // 2, M)]
         held = None
-        for t, m0, m1 in pieces:
-            if t < 3:
-                skip_part(t + 1, 1)
+        for i, (t, m0, m1) in enumerate(pieces):
+            for tt, hf in TAIL_SKIPS.get(i, ()):
+                skip_part(tt, hf)
             tiles = pair(t, m0, m1)
             if held is not None:
                 subtract(*held)
-            if t < 3:
-                second_part(t + 1, 1)
+            for tt, hf, eng in TAIL_SECONDS.get(i, ()):
+                second_part(tt, hf, eng)
             finish(t, m0, m1, *tiles)
-            held = (t, m0, m1, tiles[2])
+            held = (t, m0, m1, tiles[2], SUB[i])
             if (t, m0) == (3, M // 2):
                 cast_y(0, M // 2, "S")
         subtract(*held)

@@ -52,15 +52,13 @@ def tile_list_scaffold_lashing_features_kernel(
         tabw = [kept([P, T], I32, f"tabw{a}") for a in range(2)]
         tabs = kept([P, T], U8, "tabs")
         w2w_raw = [kept([P, 2 * N], U8, f"w2w_raw{a}") for a in range(2)]
-        late = [kept([P, 4, 256], F32, f"late{e}") for e in range(2)]
         w2s_raw = kept([P, 2, N], U8, "w2s_raw")
         gain_t = kept([P, 2, 4], F32, "gain_t")
         base_t = kept([P, 4, M], F32, "base_t")
         raw = {}
         for name in ("w10", "w11", "w3"):
             for a in range(2):
-                if (name, a) != ("w10", 1):
-                    raw[name, a] = kept([P, 4, HALF], F32, f"raw_{name}_{a}")
+                raw[name, a] = kept([P, 4, HALF], F32, f"raw_{name}_{a}")
 
         def weight_rows(name, a):
             rows = slice(HALF * a, HALF * (a + 1))
@@ -96,10 +94,7 @@ def tile_list_scaffold_lashing_features_kernel(
                 w2s_raw[32 * q : 32 * q + 4, :, :].bitcast(I32),
                 w2_scales[:, 4 * q : 4 * q + 4, :].rearrange("a r c -> r a c").bitcast(I32),
             )
-        nc.sync.dma_start(raw["w10", 0][:], weight_rows("w10", 0))
-        for e in range(2):
-            nc.sync.dma_start(late[e][:], weight_rows("w10", 1)[:, :, 256 * e : 256 * (e + 1)])
-        for name in ("w11", "w3"):
+        for name in ("w10", "w11", "w3"):
             for a in range(2):
                 nc.sync.dma_start(raw[name, a][:], weight_rows(name, a))
         nc.sync.dma_start(base_t[:], base.rearrange("(p t) m -> p t m", t=4))
@@ -108,22 +103,19 @@ def tile_list_scaffold_lashing_features_kernel(
         wq = {}
         ws = {}
 
-        def cast_columns(name, a, src, m0, m1, eng):
+        def cast_part(name, a, e, m0, m1, eng):
             if (name, a) not in grouped:
                 grouped[name, a] = stage.tile([P, 4, P, 4], BF16, name="grp", align_bytes=64)
-            dst = grouped[name, a][:, :, m0:m1, :].rearrange("p t m j -> p m j t")
-            src = src.rearrange("p j (m t) -> p m j t", t=4)
+            dst = grouped[name, a][:].rearrange("p t m j -> p m j t")[:, m0:m1, :, 2 * e : 2 * e + 2]
+            src = raw[name, a][:].rearrange("p j (m t) -> p m j t", t=4)[:, m0:m1, :, 2 * e : 2 * e + 2]
             if eng == "S":
                 nc.scalar.copy(dst, src)
-            elif eng == "V":
-                nc.vector.tensor_copy(dst, src)
             else:
-                nc.gpsimd.tensor_scalar(dst, src, 1.0, 0.0, ALU.mult, ALU.add)
+                nc.vector.tensor_copy(dst, src)
 
         def cast_weight(name, a, engs):
-            w = P // len(engs)
             for e, eng in enumerate(engs):
-                cast_columns(name, a, raw[name, a][:, :, 4 * w * e : 4 * w * (e + 1)], w * e, w * (e + 1), eng)
+                cast_part(name, a, e, 0, P, eng)
 
         def quant_weight(name, a):
             wq[name, a] = kept([P, HALF], U32, f"wq_{name}_{a}")
@@ -138,7 +130,7 @@ def tile_list_scaffold_lashing_features_kernel(
         w2s = kept([P, 2, 4, P], U8, "w2s")
         for a in range(2):
             nc.vector.tensor_copy(
-                w2w[:, a].rearrange("p t q e -> p q t e"), w2w_raw[a][:].rearrange("p (q t e) -> p q t e", t=4, e=2)
+                w2w[:, a], w2w_raw[a][:].rearrange("p (q t e) -> p t q e", t=4, e=2)
             )
 
         gain_w = kept([P, 2, CH, 4], F32, "gain_w")
@@ -165,14 +157,14 @@ def tile_list_scaffold_lashing_features_kernel(
         nc.vector.tensor_copy(vs[:], tabs[:].indirect(offs_t[:]))
         gather_words(1, 0)
         gather_words(1, 1)
-        cast_weight("w10", 0, "S")
+        cast_weight("w10", 0, "SS")
         quant_weight("w10", 0)
-        cast_columns("w10", 1, late[0][:], 0, 64, "V")
-        cast_columns("w10", 1, late[1][:, :, 0:160], 64, 104, "V")
-        cast_columns("w10", 1, late[1][:, :, 160:256], 104, 128, "S")
+        cast_part("w10", 1, 0, 0, P, "V")
+        cast_part("w10", 1, 1, 0, 40, "V")
+        cast_part("w10", 1, 1, 40, P, "S")
         quant_weight("w10", 1)
         nc.vector.tensor_copy(
-            w2s[:].rearrange("p a t q -> p a q t"), w2s_raw[:].rearrange("p a (q t) -> p a q t", t=4)
+            w2s[:], w2s_raw[:].rearrange("p a (q t) -> p a t q", t=4)
         )
 
         hq = {}
@@ -191,16 +183,16 @@ def tile_list_scaffold_lashing_features_kernel(
             hf, c0 = divmod(c * CH, HALF)
             name = "w10" if b == 0 else "w11"
             bank = psum.tile([P, 4, CH], F32, name="bank", tag="bank")
-            for t in range(4):
-                for a in range(2):
+            for a in range(2):
+                for t in range(4):
                     nc.tensor.matmul_mx(
                         out=bank[:, t, :],
                         lhsT=wq[name, a][:, P * t : P * (t + 1)].bitcast(E4M3),
                         lhsT_scale=ws[name, a][:, P * t : P * (t + 1)],
                         rhs=vw[a, hf][:, c0 : c0 + CH].bitcast(E4M3),
                         rhs_scale=vs[4 * a : P, c * CH : (c + 1) * CH],
-                        start=(a == 0),
-                        stop=(a == 1),
+                        start=(a, t) == (0, 0),
+                        stop=(a, t) == (1, 3),
                     )
             woven = bank[:].rearrange("p t n -> p n t")
             sine = ring.tile([P, CH, 4], F32, name="sine")
@@ -213,7 +205,7 @@ def tile_list_scaffold_lashing_features_kernel(
         def apply_gain(u):
             b, c = units[u]
             if u % 2 == 0:
-                hb[u // 2] = ring.tile([P, 2, CH, 4], BF16, name="hb", align_bytes=64)
+                hb[u // 2] = ring.tile([P, 2, CH, 4], BF16, name="hb", align_bytes=64, bufs=2)
             if GAIN[u] == "G":
                 nc.gpsimd.tensor_tensor(hb[u // 2][:, u % 2], diff[u][:], gain_w[:, b], ALU.mult)
             else:
@@ -275,8 +267,8 @@ def tile_list_scaffold_lashing_features_kernel(
                 first_half(u)
             if 1 <= u <= last + 1:
                 apply_gain(u - 1)
-            if u >= 3 and u % 2 == 1:
-                quant_h(u - 3)
+            if u >= 2 and u % 2 == 0:
+                quant_h(u - 2)
             for (name, a), (when, engs) in CASTS.items():
                 if u == when:
                     cast_weight(name, a, engs)

@@ -19,15 +19,9 @@ ACT = mybir.ActivationFunctionType
 ALU = mybir.AluOpType
 
 P = 128
-HALF = 512
+PASS = 512
+BANK = 512
 CH = 128
-GAIN = "GVGVGVGVGVGVGVGV"
-CASTS = {("w11", 0): (0, "VV"), ("w11", 1): (3, "SV"), ("w3", 0): (7, "SV"), ("w3", 1): (9, "SV")}
-SKIPS = {12: [(0, 0)], 13: [(1, 0)], 15: [(0, 1)]}
-SECONDS = {15: [(0, 0)], 16: [(1, 0)], 17: [(0, 1)]}
-TAIL_SKIPS = {0: [(1, 1), (2, 0)], 1: [(2, 1), (3, 0)], 2: [(3, 1)]}
-TAIL_SECONDS = {0: [(1, 1, "V"), (2, 0, "G")], 1: [(2, 1, "V"), (3, 0, "G")], 2: [(3, 1, "V")]}
-SUB = "GGGGV"
 
 
 def tile_list_scaffold_lashing_features_kernel(
@@ -36,9 +30,7 @@ def tile_list_scaffold_lashing_features_kernel(
     nc = tc.nc
     with ExitStack() as ctx:
         keep = ctx.enter_context(tc.tile_pool(name="keep", bufs=1))
-        ring = ctx.enter_context(tc.tile_pool(name="ring", bufs=4))
-        stage = ctx.enter_context(tc.tile_pool(name="stage", bufs=3))
-        tail = ctx.enter_context(tc.tile_pool(name="tail", bufs=2))
+        ring = ctx.enter_context(tc.tile_pool(name="ring", bufs=2))
         psum = ctx.enter_context(tc.psum_pool(name="psum", bufs=7))
         psum_keep = ctx.enter_context(tc.psum_pool(name="psum_keep", bufs=1))
 
@@ -48,90 +40,55 @@ def tile_list_scaffold_lashing_features_kernel(
         offs_t = keep.tile([P, S // 16], U16, name="offs_t")
         pos1_t = keep.tile([P, M // 16], U16, name="pos1_t")
         pos2_t = keep.tile([P, M // 16], U16, name="pos2_t")
-
         tabw = [kept([P, T], I32, f"tabw{a}") for a in range(2)]
         tabs = kept([P, T], U8, "tabs")
-        w2w_raw = [kept([P, 2 * N], U8, f"w2w_raw{a}") for a in range(2)]
+        w2w_raw = [kept([P, 2 * N], U8, f"w2w_raw{b}") for b in range(2)]
         w2s_raw = kept([P, 2, N], U8, "w2s_raw")
         gain_t = kept([P, 2, 4], F32, "gain_t")
         base_t = kept([P, 4, M], F32, "base_t")
-        raw = {}
-        for name in ("w10", "w11", "w3"):
-            for a in range(2):
-                raw[name, a] = kept([P, 4, HALF], F32, f"raw_{name}_{a}")
-
-        def weight_rows(name, a):
-            rows = slice(HALF * a, HALF * (a + 1))
-            if name == "w3":
-                src = w3[rows, :]
-            else:
-                b = 0 if name == "w10" else 1
-                src = w1[rows, HALF * b : HALF * (b + 1)]
-            return src.rearrange("(p j) c -> p j c", j=4)
+        sources = [w1[:, 0:PASS], w1[:, PASS : 2 * PASS], w3]
+        raw = [[kept([P, 4, PASS], F32, f"raw{w}{a}") for a in range(2)] for w in range(3)]
 
         warm = keep.tile([P, 2], F32, name="warm")
         nc.gpsimd.memset(warm[:, 0:1], 0.0)
         nc.scalar.activation(warm[:, 1:2], warm[:, 0:1], ACT.Sin)
         nc.vector.memset(tabs[:].bitcast(I32), 0)
-        nc.gpsimd.memset(w2s_raw[:].rearrange("p a c -> p (a c)").bitcast(I32), 0)
+        nc.gpsimd.memset(w2s_raw[:].rearrange("p b c -> p (b c)").bitcast(I32), 0)
 
+        def load_weight(w, a):
+            rows = sources[w][PASS * a : PASS * (a + 1), :]
+            nc.sync.dma_start(raw[w][a][:], rows.rearrange("(p j) c -> p j c", j=4))
+
+        words = [tab_words[a].rearrange("p t i -> p (t i)").bitcast(I32) for a in range(2)]
+        nc.sync.dma_start(tabw[0][:, 0 : T // 2], words[0][:, 0 : T // 2])
         nc.sync.dma_start(offs_t[:], offs)
         nc.sync.dma_start(pos1_t[:], pos1)
         nc.sync.dma_start(pos2_t[:], pos2)
         nc.sync.dma_start(gain_t[:], gain.rearrange("(b p t) -> p b t", b=2, t=4))
-        for a in range(2):
-            nc.sync.dma_start(w2w_raw[a][:].bitcast(I32), w2_words[a].bitcast(I32))
-        words = [tab_words[a].rearrange("p t i -> p (t i)").bitcast(I32) for a in range(2)]
-        for c0 in (0, T // 2):
-            nc.sync.dma_start(tabw[0][:, c0 : c0 + T // 2], words[0][:, c0 : c0 + T // 2])
-        for q in range(4):
+        for b in range(2):
+            nc.sync.dma_start(w2w_raw[b][:].bitcast(I32), w2_words[b].bitcast(I32))
+        nc.sync.dma_start(tabw[0][:, T // 2 : T], words[0][:, T // 2 : T])
+        for q in (0, 2, 1, 3):
             nc.sync.dma_start(
                 tabs[32 * q : 32 * q + 8, :].bitcast(I32), tab_scales[:, 4 * q : 4 * q + 4, :].bitcast(I32)
             )
-        nc.sync.dma_start(tabw[1][:], words[1])
-        for q in range(4):
+        for a in range(2):
+            load_weight(0, a)
+        for q in (0, 2, 1, 3):
             nc.sync.dma_start(
                 w2s_raw[32 * q : 32 * q + 4, :, :].bitcast(I32),
-                w2_scales[:, 4 * q : 4 * q + 4, :].rearrange("a r c -> r a c").bitcast(I32),
+                w2_scales[:, 4 * q : 4 * q + 4, :].rearrange("b r c -> r b c").bitcast(I32),
             )
-        for name in ("w10", "w11", "w3"):
+        nc.sync.dma_start(tabw[1][:], words[1])
+        for w in (1, 2):
             for a in range(2):
-                nc.sync.dma_start(raw[name, a][:], weight_rows(name, a))
+                load_weight(w, a)
         nc.sync.dma_start(base_t[:], base.rearrange("(p t) m -> p t m", t=4))
-
-        grouped = {}
-        wq = {}
-        ws = {}
-
-        def cast_part(name, a, e, m0, m1, eng):
-            if (name, a) not in grouped:
-                grouped[name, a] = stage.tile([P, 4, P, 4], BF16, name="grp", align_bytes=64)
-            dst = grouped[name, a][:].rearrange("p t m j -> p m j t")[:, m0:m1, :, 2 * e : 2 * e + 2]
-            src = raw[name, a][:].rearrange("p j (m t) -> p m j t", t=4)[:, m0:m1, :, 2 * e : 2 * e + 2]
-            if eng == "S":
-                nc.scalar.copy(dst, src)
-            else:
-                nc.vector.tensor_copy(dst, src)
-
-        def cast_weight(name, a, engs):
-            for e, eng in enumerate(engs):
-                cast_part(name, a, e, 0, P, eng)
-
-        def quant_weight(name, a):
-            wq[name, a] = kept([P, HALF], U32, f"wq_{name}_{a}")
-            ws[name, a] = kept([P, HALF], U8, f"ws_{name}_{a}")
-            nc.vector.quantize_mx(
-                out=wq[name, a][:].bitcast(E4M3),
-                scales=ws[name, a][:],
-                in_=grouped[name, a][:].rearrange("p t m j -> p (t m j)"),
-            )
 
         w2w = kept([P, 2, 4, P, 2], U8, "w2w")
         w2s = kept([P, 2, 4, P], U8, "w2s")
-        for a in range(2):
-            nc.vector.tensor_copy(
-                w2w[:, a], w2w_raw[a][:].rearrange("p (q t e) -> p t q e", t=4, e=2)
-            )
+        for b in range(2):
+            nc.vector.tensor_copy(w2w[:, b], w2w_raw[b][:].rearrange("p (q t e) -> p t q e", t=4, e=2))
 
         gain_w = kept([P, 2, CH, 4], F32, "gain_w")
         nc.vector.tensor_copy(gain_w[:], gain_t[:].unsqueeze(2).to_broadcast([P, 2, CH, 4]))
@@ -145,199 +102,212 @@ def tile_list_scaffold_lashing_features_kernel(
         gain_bank = psum_keep.tile([P, 2, P], F32, name="gain_bank")
         for b in range(2):
             nc.tensor.transpose(gain_bank[:, b, :], gain_rows[:, b, :], ident[:])
-        vs = kept([P, S], U8, "vs")
-        vw = {}
+
+        rounded = [
+            [ring.tile([P, 4, P, 4], BF16, name="rounded", align_bytes=64, bufs=4) for a in range(2)] for w in range(3)
+        ]
+        wq = [[kept([P, PASS], U32, f"wq{w}{a}") for a in range(2)] for w in range(3)]
+        ws = [[kept([P, PASS], U8, f"ws{w}{a}") for a in range(2)] for w in range(3)]
+
+        def round_weight(copy, w, a, t0, t1, m0=0, m1=P):
+            copy(
+                rounded[w][a][:, t0:t1, m0:m1, :].rearrange("p t m j -> p m j t"),
+                raw[w][a][:].rearrange("p j (m t) -> p m j t", t=4)[:, m0:m1, :, t0:t1],
+            )
+
+        def quantise_weight(w, a, t0, t1):
+            nc.vector.quantize_mx(
+                out=wq[w][a][:, P * t0 : P * t1].bitcast(E4M3),
+                scales=ws[w][a][:, P * t0 : P * t1],
+                in_=rounded[w][a][:, t0:t1].rearrange("p t m j -> p (t m j)"),
+            )
+
+        vw = [[kept([P, BANK], U32, f"vw{a}{hf}") for hf in range(2)] for a in range(2)]
 
         def gather_words(a, hf):
-            vw[a, hf] = kept([P, HALF], U32, f"vw{a}{hf}")
-            nc.vector.tensor_copy(vw[a, hf][:], tabw[a][:].bitcast(U32).indirect(offs_t[:, 32 * hf : 32 * (hf + 1)]))
+            nc.vector.tensor_copy(vw[a][hf][:], tabw[a][:].bitcast(U32).indirect(offs_t[:, 32 * hf : 32 * (hf + 1)]))
 
         gather_words(0, 0)
         gather_words(0, 1)
+        vs = kept([P, S], U8, "vs")
         nc.vector.tensor_copy(vs[:], tabs[:].indirect(offs_t[:]))
+        for a in range(2):
+            round_weight(nc.scalar.copy, 0, a, 0, 4)
+            quantise_weight(0, a, 0, 4)
+        nc.vector.tensor_copy(w2s[:], w2s_raw[:].rearrange("p b (q t) -> p b t q", t=4))
         gather_words(1, 0)
         gather_words(1, 1)
-        cast_weight("w10", 0, "SS")
-        quant_weight("w10", 0)
-        cast_part("w10", 1, 0, 0, P, "V")
-        cast_part("w10", 1, 1, 0, 40, "V")
-        cast_part("w10", 1, 1, 40, P, "S")
-        quant_weight("w10", 1)
-        nc.vector.tensor_copy(
-            w2s[:], w2s_raw[:].rearrange("p a (q t) -> p a t q", t=4)
-        )
 
-        hq = {}
-        hs = {}
-        for b in range(2):
-            for hf in range(2):
-                hq[b, hf] = kept([P, HALF], U32, f"hq{b}{hf}")
-                hs[b, hf] = kept([P, HALF], U8, f"hs{b}{hf}")
+        hq = [[kept([P, BANK], U32, f"hq{b}{hf}") for hf in range(2)] for b in range(2)]
+        hs = [[kept([P, BANK], U8, f"hs{b}{hf}") for hf in range(2)] for b in range(2)]
+        g2 = [kept([P, S], F32, f"g2_{t}") for t in range(4)]
 
-        units = [(b, c) for b in range(2) for c in range(S // CH)]
-        diff = {}
-        hb = {}
-
-        def first_half(u):
-            b, c = units[u]
-            hf, c0 = divmod(c * CH, HALF)
-            name = "w10" if b == 0 else "w11"
+        def response(b, c):
+            hf, c0 = divmod(CH * c, BANK)
             bank = psum.tile([P, 4, CH], F32, name="bank", tag="bank")
             for a in range(2):
                 for t in range(4):
                     nc.tensor.matmul_mx(
                         out=bank[:, t, :],
-                        lhsT=wq[name, a][:, P * t : P * (t + 1)].bitcast(E4M3),
-                        lhsT_scale=ws[name, a][:, P * t : P * (t + 1)],
-                        rhs=vw[a, hf][:, c0 : c0 + CH].bitcast(E4M3),
-                        rhs_scale=vs[4 * a : P, c * CH : (c + 1) * CH],
+                        lhsT=wq[b][a][:, P * t : P * (t + 1)].bitcast(E4M3),
+                        lhsT_scale=ws[b][a][:, P * t : P * (t + 1)],
+                        rhs=vw[a][hf][:, c0 : c0 + CH].bitcast(E4M3),
+                        rhs_scale=vs[4 * a : P, CH * c : CH * (c + 1)],
                         start=(a, t) == (0, 0),
                         stop=(a, t) == (1, 3),
                     )
             woven = bank[:].rearrange("p t n -> p n t")
-            sine = ring.tile([P, CH, 4], F32, name="sine")
+            sine = ring.tile([P, CH, 4], F32, name="sine", bufs=3)
             nc.scalar.activation(sine[:], woven, ACT.Sin, scale=0.5)
-            versine = ring.tile([P, CH, 4], F32, name="versine")
+            versine = ring.tile([P, CH, 4], F32, name="versine", bufs=4)
             nc.scalar.activation(versine[:], sine[:], ACT.Square, scale=math.sqrt(2.0))
-            diff[u] = ring.tile([P, CH, 4], F32, name="diff")
-            nc.vector.scalar_tensor_tensor(diff[u][:], woven, -1.0, versine[:], ALU.add, ALU.add)
+            diff = ring.tile([P, CH, 4], F32, name="diff", bufs=4)
+            nc.vector.scalar_tensor_tensor(diff[:], woven, -1.0, versine[:], ALU.add, ALU.add)
+            return diff
 
-        def apply_gain(u):
-            b, c = units[u]
-            if u % 2 == 0:
-                hb[u // 2] = ring.tile([P, 2, CH, 4], BF16, name="hb", align_bytes=64, bufs=2)
-            if GAIN[u] == "G":
-                nc.gpsimd.tensor_tensor(hb[u // 2][:, u % 2], diff[u][:], gain_w[:, b], ALU.mult)
-            else:
-                nc.vector.tensor_tensor(
-                    hb[u // 2][:, u % 2].rearrange("p (r n) t -> p r (n t)", r=4),
-                    diff[u][:].rearrange("p (r n) t -> p r (n t)", r=4),
-                    gain_bank[:, b : b + 1, :].to_broadcast([P, 4, P]),
-                    ALU.mult,
-                )
+        def gain_on_gpsimd(dst, diff, b, n0, n1):
+            nc.gpsimd.tensor_tensor(dst[:, n0:n1], diff[:, n0:n1], gain_w[:, b, n0:n1], ALU.mult)
 
-        def quant_h(u):
-            b, c = units[u]
-            hf, c0 = divmod(c * CH, HALF)
-            nc.vector.quantize_mx(
-                out=hq[b, hf][:, c0 : c0 + 2 * CH].bitcast(E4M3),
-                scales=hs[b, hf][:, c0 : c0 + 2 * CH],
-                in_=hb[u // 2][:].rearrange("p e n t -> p (e n t)"),
+        def gain_on_vector(dst, diff, b, n0, n1):
+            nc.vector.tensor_tensor(
+                dst[:, n0:n1].rearrange("p (r n) t -> p r (n t)", n=32),
+                diff[:, n0:n1].rearrange("p (r n) t -> p r (n t)", n=32),
+                gain_bank[:, b : b + 1, :].to_broadcast([P, (n1 - n0) // 32, P]),
+                ALU.mult,
             )
 
-        g2 = [kept([P, S], F32, f"g2_{t}") for t in range(4)]
+        def hidden(b, c):
+            h_round = ring.tile([P, 2, CH, 4], BF16, name="h_round", align_bytes=64)
+            gain_on_gpsimd(h_round[:, 0], response(b, c), b, 0, CH)
+            diff = response(b, c + 1)
+            gain_on_vector(h_round[:, 1], diff, b, 0, CH)
+            hf, c0 = divmod(CH * c, BANK)
+            nc.vector.quantize_mx(
+                out=hq[b][hf][:, c0 : c0 + 2 * CH].bitcast(E4M3),
+                scales=hs[b][hf][:, c0 : c0 + 2 * CH],
+                in_=h_round[:].rearrange("p e n t -> p (e n t)"),
+            )
 
-        def skip_part(t, hf):
-            bank = psum.tile([P, HALF], F32, name="bank", tag="bank")
+        def skip_size(t, hf):
+            bank = psum.tile([P, BANK], F32, name="bank", tag="bank")
             for a in range(2):
                 nc.tensor.matmul_mx(
                     out=bank[:],
-                    lhsT=wq["w3", a][:, P * t : P * (t + 1)].bitcast(E4M3),
-                    lhsT_scale=ws["w3", a][:, P * t : P * (t + 1)],
-                    rhs=vw[a, hf][:].bitcast(E4M3),
-                    rhs_scale=vs[4 * a : P, HALF * hf : HALF * (hf + 1)],
+                    lhsT=wq[2][a][:, P * t : P * (t + 1)].bitcast(E4M3),
+                    lhsT_scale=ws[2][a][:, P * t : P * (t + 1)],
+                    rhs=vw[a][hf][:].bitcast(E4M3),
+                    rhs_scale=vs[4 * a : P, BANK * hf : BANK * (hf + 1)],
                     start=(a == 0),
                     stop=(a == 1),
                 )
-            nc.scalar.activation(g2[t][:, HALF * hf : HALF * (hf + 1)], bank[:], ACT.Abs)
+            nc.scalar.activation(g2[t][:, BANK * hf : BANK * (hf + 1)], bank[:], ACT.Abs)
 
-        def second_part(t, hf, on="V"):
-            bank = psum.tile([P, HALF], F32, name="bank", tag="bank")
+        def add_features(t, hf, by_gpsimd):
+            bank = psum.tile([P, BANK], F32, name="bank", tag="bank")
             for b in range(2):
                 nc.tensor.matmul_mx(
                     out=bank[:],
                     lhsT=w2w[:, b, t].rearrange("p q e -> p (q e)").bitcast(E2M1),
                     lhsT_scale=w2s[:, b, t, :],
-                    rhs=hq[b, hf][:].bitcast(E4M3),
-                    rhs_scale=hs[b, hf][:],
+                    rhs=hq[b][hf][:].bitcast(E4M3),
+                    rhs_scale=hs[b][hf][:],
                     start=(b == 0),
                     stop=(b == 1),
                 )
-            cols = slice(HALF * hf, HALF * (hf + 1))
-            if on == "V":
-                nc.vector.tensor_tensor(g2[t][:, cols], bank[:], g2[t][:, cols], ALU.add)
-            else:
-                part = tail.tile([P, HALF], F32, name="part")
+            dst = g2[t][:, BANK * hf : BANK * (hf + 1)]
+            if by_gpsimd:
+                part = ring.tile([P, BANK], F32, name="part")
                 nc.scalar.copy(part[:], bank[:])
-                nc.gpsimd.tensor_tensor(g2[t][:, cols], part[:], g2[t][:, cols], ALU.add)
+                nc.gpsimd.tensor_tensor(dst, part[:], dst, ALU.add)
+            else:
+                nc.vector.tensor_tensor(dst, bank[:], dst, ALU.add)
 
-        last = len(units) - 1
-        for u in range(len(units) + 2):
-            if u <= last:
-                first_half(u)
-            if 1 <= u <= last + 1:
-                apply_gain(u - 1)
-            if u >= 2 and u % 2 == 0:
-                quant_h(u - 2)
-            for (name, a), (when, engs) in CASTS.items():
-                if u == when:
-                    cast_weight(name, a, engs)
-                if u == when + 1:
-                    quant_weight(name, a)
-            for t, hf in SKIPS.get(u, ()):
-                skip_part(t, hf)
-            for t, hf in SECONDS.get(u, ()):
-                second_part(t, hf)
+        round_weight(nc.vector.tensor_copy, 1, 0, 0, 2)
+        round_weight(nc.vector.tensor_copy, 1, 0, 2, 4)
+        quantise_weight(1, 0, 0, 4)
+        hidden(0, 0)
+        hidden(0, 2)
+        round_weight(nc.scalar.copy, 1, 1, 0, 2)
+        round_weight(nc.vector.tensor_copy, 1, 1, 2, 4)
+        quantise_weight(1, 1, 0, 4)
+        hidden(0, 4)
+        hidden(0, 6)
+        round_weight(nc.scalar.copy, 2, 0, 0, 2)
+        quantise_weight(2, 0, 0, 2)
+        hidden(1, 0)
+        round_weight(nc.scalar.copy, 2, 1, 0, 2)
+        quantise_weight(2, 1, 0, 2)
+        hidden(1, 2)
+        hidden(1, 4)
+        skip_size(0, 0)
+        add_features(0, 0, False)
+        hidden(1, 6)
+        skip_size(0, 1)
+        skip_size(1, 0)
+        add_features(1, 0, False)
+        add_features(0, 1, False)
+        skip_size(1, 1)
+        for a in range(2):
+            round_weight(nc.scalar.copy, 2, a, 2, 4)
+            quantise_weight(2, a, 2, 4)
 
         y = kept([P, 4, M], F32, "y")
-        out0_v = out_0.rearrange("(p t) m -> p t m", t=4)
-
-        def pair(t, m0, m1):
-            w = m1 - m0
-            left = tail.tile([P, w], F32, name="left")
-            right = tail.tile([P, w], F32, name="right")
-            larger = tail.tile([P, w], F32, name="larger")
-            nc.vector.tensor_copy(left[:], g2[t][:].indirect(pos1_t[:, m0 // 16 : m1 // 16]))
-            nc.vector.tensor_copy(right[:], g2[t][:].indirect(pos2_t[:, m0 // 16 : m1 // 16]))
-            return left, right, larger
-
-        def finish(t, m0, m1, left, right, larger):
-            nc.vector.tensor_tensor(larger[:], left[:], right[:], ALU.max)
-
-        def subtract(t, m0, m1, larger, on):
-            eng = nc.vector if on == "V" else nc.gpsimd
-            eng.tensor_tensor(y[:, t, m0:m1], larger[:], base_t[:, t, m0:m1], ALU.subtract)
-            nc.sync.dma_start(out0_v[:, t, m0:m1], y[:, t, m0:m1])
-
         yq = kept([P, M], U32, "yq")
         ys = kept([P, M], U8, "ys")
-        yb = {}
+        out0_rows = out_0.rearrange("(p t) m -> p t m", t=4)
+        out1_words = out_1[0].rearrange("p m t -> p (m t)").bitcast(I32)
 
-        def cast_y(m0, m1, eng):
-            yb[m0] = kept([P, m1 - m0, 4], BF16, f"yb{m0}")
-            dst = yb[m0][:].rearrange("p (c i) t -> p c t i", i=4)
-            src = y[:, :, m0:m1].rearrange("p t (c i) -> p c t i", i=4)
-            if eng == "S":
-                nc.scalar.copy(dst, src)
+        def turned_copy(src, name, scale):
+            bank = psum.tile([P, 4, P], F32, name="bank", tag="bank")
+            for i in range(4):
+                nc.tensor.transpose(bank[:, i, :], src[:, P * i : P * (i + 1)], ident[:])
+            dst = ring.tile([P, 4, P], F32, name=name)
+            nc.scalar.activation(dst[:], bank[:], ACT.Copy, scale=scale)
+            return dst
+
+        def subtract_on_tensor(t, larger):
+            base_turned = turned_copy(base_t[:, t, :], "base_turned", -1.0)
+            larger_turned = turned_copy(larger, "larger_turned", 1.0)
+            bank = psum.tile([P, 4, P], F32, name="bank", tag="bank")
+            for i in range(4):
+                nc.tensor.matmul(bank[:, i, :], base_turned[:, i, :], ident[:], start=True, stop=False, is_transpose=True)
+                nc.tensor.matmul(bank[:, i, :], larger_turned[:, i, :], ident[:], start=False, stop=True, is_transpose=True)
+            nc.scalar.copy(y[:, t, :], bank[:].rearrange("p i m -> p (i m)"))
+
+        def joints(t, m0, m1, engine):
+            left = ring.tile([P, m1 - m0], F32, name="left")
+            right = ring.tile([P, m1 - m0], F32, name="right")
+            larger = ring.tile([P, m1 - m0], F32, name="larger")
+            nc.vector.tensor_copy(left[:], g2[t][:].indirect(pos1_t[:, m0 // 16 : m1 // 16]))
+            nc.vector.tensor_copy(right[:], g2[t][:].indirect(pos2_t[:, m0 // 16 : m1 // 16]))
+            nc.vector.tensor_tensor(larger[:], left[:], right[:], ALU.max)
+            if engine is None:
+                subtract_on_tensor(t, larger[:])
             else:
-                nc.vector.tensor_copy(dst, src)
+                engine.tensor_tensor(y[:, t, m0:m1], larger[:], base_t[:, t, m0:m1], ALU.subtract)
+            nc.sync.dma_start(out0_rows[:, t, m0:m1], y[:, t, m0:m1])
 
-        def quant_y(m0, m1):
+        def planes(copy, m0, m1):
+            y_round = ring.tile([P, m1 - m0, 4], BF16, name="y_round", align_bytes=64)
+            copy(
+                y_round[:].rearrange("p (c i) t -> p c t i", i=4), y[:, :, m0:m1].rearrange("p t (c i) -> p c t i", i=4)
+            )
             nc.vector.quantize_mx(
-                out=yq[:, m0:m1].bitcast(E4M3), scales=ys[:, m0:m1], in_=yb[m0][:].rearrange("p m t -> p (m t)")
+                out=yq[:, m0:m1].bitcast(E4M3), scales=ys[:, m0:m1], in_=y_round[:].rearrange("p m t -> p (m t)")
             )
-            nc.scalar.dma_start(
-                out_1[0].rearrange("p m t -> p (m t)").bitcast(I32)[:, m0:m1], yq[:, m0:m1].bitcast(I32)
-            )
+            nc.scalar.dma_start(out1_words[:, m0:m1], yq[:, m0:m1].bitcast(I32))
 
-        pieces = [(0, 0, M), (1, 0, M), (2, 0, M), (3, 0, M // 2), (3, M // 2, M)]
-        held = None
-        for i, (t, m0, m1) in enumerate(pieces):
-            for tt, hf in TAIL_SKIPS.get(i, ()):
-                skip_part(tt, hf)
-            tiles = pair(t, m0, m1)
-            if held is not None:
-                subtract(*held)
-            for tt, hf, eng in TAIL_SECONDS.get(i, ()):
-                second_part(tt, hf, eng)
-            finish(t, m0, m1, *tiles)
-            held = (t, m0, m1, tiles[2], SUB[i])
-            if (t, m0) == (3, M // 2):
-                cast_y(0, M // 2, "S")
-        subtract(*held)
-        quant_y(0, M // 2)
-        cast_y(M // 2, M, "V")
-        quant_y(M // 2, M)
+        add_features(1, 1, False)
+        for t in range(3):
+            if t < 2:
+                for hf in range(2):
+                    skip_size(t + 2, hf)
+                    add_features(t + 2, hf, False)
+            joints(t, 0, M, None)
+        joints(3, 0, M // 2, nc.vector)
+        joints(3, M // 2, M, nc.vector)
+        planes(nc.scalar.copy, 0, M // 2)
+        planes(nc.vector.tensor_copy, M // 2, M)
         for q in range(4):
-            eng = nc.sync if q % 2 == 0 else nc.scalar
-            eng.dma_start(out_2[0, 4 * q : 4 * q + 4, :].bitcast(I32), ys[32 * q : 32 * q + 4, :].bitcast(I32))
+            queue = nc.sync if q % 2 == 0 else nc.scalar
+            queue.dma_start(out_2[0, 4 * q : 4 * q + 4, :].bitcast(I32), ys[32 * q : 32 * q + 4, :].bitcast(I32))

@@ -21,13 +21,17 @@ ALU = mybir.AluOpType
 P = 128
 PASS = 512
 BANK = 512
-CH = 128
+CHUNK = 128
+PER_COLUMN = 16
+QUADRANTS = (0, 2, 1, 3)
+W1_LOW, W1_HIGH, W3 = 0, 1, 2
 
 
 def tile_list_scaffold_lashing_features_kernel(
     tc, tab_words, tab_scales, offs, pos1, pos2, w1, gain, w2_words, w2_scales, w3, base, out_0, out_1, out_2
 ):
     nc = tc.nc
+    on_vector, on_scalar = nc.vector.tensor_copy, nc.scalar.copy
     with ExitStack() as ctx:
         keep = ctx.enter_context(tc.tile_pool(name="keep", bufs=1))
         ring = ctx.enter_context(tc.tile_pool(name="ring", bufs=2))
@@ -37,228 +41,236 @@ def tile_list_scaffold_lashing_features_kernel(
         def kept(shape, dtype, name):
             return keep.tile(shape, dtype, name=name, align_bytes=64)
 
-        offs_t = keep.tile([P, S // 16], U16, name="offs_t")
-        pos1_t = keep.tile([P, M // 16], U16, name="pos1_t")
-        pos2_t = keep.tile([P, M // 16], U16, name="pos2_t")
-        tabw = [kept([P, T], I32, f"tabw{a}") for a in range(2)]
-        tabs = kept([P, T], U8, "tabs")
-        w2w_raw = [kept([P, 2 * N], U8, f"w2w_raw{b}") for b in range(2)]
-        w2s_raw = kept([P, 2, N], U8, "w2s_raw")
+        def new_bank(shape):
+            return psum.tile(shape, F32, name="bank", tag="bank")
+
+        offs_t = keep.tile([P, S // PER_COLUMN], U16, name="offs_t")
+        pos1_t = keep.tile([P, M // PER_COLUMN], U16, name="pos1_t")
+        pos2_t = keep.tile([P, M // PER_COLUMN], U16, name="pos2_t")
+        table_words = [kept([P, T], I32, f"table_words{a}") for a in range(2)]
+        table_scales = kept([P, T], U8, "table_scales")
+        w2_words_raw = [kept([P, 2 * N], U8, f"w2_words_raw{b}") for b in range(2)]
+        w2_scales_raw = kept([P, 2, N], U8, "w2_scales_raw")
         gain_t = kept([P, 2, 4], F32, "gain_t")
         base_t = kept([P, 4, M], F32, "base_t")
-        sources = [w1[:, 0:PASS], w1[:, PASS : 2 * PASS], w3]
+        weights = [w1[:, 0:PASS], w1[:, PASS : 2 * PASS], w3]
         raw = [[kept([P, 4, PASS], F32, f"raw{w}{a}") for a in range(2)] for w in range(3)]
 
-        warm = keep.tile([P, 2], F32, name="warm")
-        nc.gpsimd.memset(warm[:, 0:1], 0.0)
-        nc.scalar.activation(warm[:, 1:2], warm[:, 0:1], ACT.Sin)
-        nc.vector.memset(tabs[:].bitcast(I32), 0)
-        nc.gpsimd.memset(w2s_raw[:].rearrange("p b c -> p (b c)").bitcast(I32), 0)
+        nc.vector.memset(table_scales[:].bitcast(I32), 0)
+        nc.gpsimd.memset(w2_scales_raw[:].rearrange("p b c -> p (b c)").bitcast(I32), 0)
 
         def load_weight(w, a):
-            rows = sources[w][PASS * a : PASS * (a + 1), :]
+            rows = weights[w][PASS * a : PASS * (a + 1), :]
             nc.sync.dma_start(raw[w][a][:], rows.rearrange("(p j) c -> p j c", j=4))
 
         words = [tab_words[a].rearrange("p t i -> p (t i)").bitcast(I32) for a in range(2)]
-        nc.sync.dma_start(tabw[0][:, 0 : T // 2], words[0][:, 0 : T // 2])
+        nc.sync.dma_start(table_words[0][:, 0 : T // 2], words[0][:, 0 : T // 2])
         nc.sync.dma_start(offs_t[:], offs)
         nc.sync.dma_start(pos1_t[:], pos1)
         nc.sync.dma_start(pos2_t[:], pos2)
         nc.sync.dma_start(gain_t[:], gain.rearrange("(b p t) -> p b t", b=2, t=4))
         for b in range(2):
-            nc.sync.dma_start(w2w_raw[b][:].bitcast(I32), w2_words[b].bitcast(I32))
-        nc.sync.dma_start(tabw[0][:, T // 2 : T], words[0][:, T // 2 : T])
-        for q in (0, 2, 1, 3):
+            nc.sync.dma_start(w2_words_raw[b][:].bitcast(I32), w2_words[b].bitcast(I32))
+        nc.sync.dma_start(table_words[0][:, T // 2 : T], words[0][:, T // 2 : T])
+        for q in QUADRANTS:
             nc.sync.dma_start(
-                tabs[32 * q : 32 * q + 8, :].bitcast(I32), tab_scales[:, 4 * q : 4 * q + 4, :].bitcast(I32)
+                table_scales[32 * q : 32 * q + 8, :].bitcast(I32), tab_scales[:, 4 * q : 4 * q + 4, :].bitcast(I32)
             )
         for a in range(2):
-            load_weight(0, a)
-        for q in (0, 2, 1, 3):
+            load_weight(W1_LOW, a)
+        for q in QUADRANTS:
             nc.sync.dma_start(
-                w2s_raw[32 * q : 32 * q + 4, :, :].bitcast(I32),
+                w2_scales_raw[32 * q : 32 * q + 4, :, :].bitcast(I32),
                 w2_scales[:, 4 * q : 4 * q + 4, :].rearrange("b r c -> r b c").bitcast(I32),
             )
-        nc.sync.dma_start(tabw[1][:], words[1])
-        for w in (1, 2):
+        nc.sync.dma_start(table_words[1][:], words[1])
+        for w in (W1_HIGH, W3):
             for a in range(2):
                 load_weight(w, a)
         nc.sync.dma_start(base_t[:], base.rearrange("(p t) m -> p t m", t=4))
 
-        w2w = kept([P, 2, 4, P, 2], U8, "w2w")
-        w2s = kept([P, 2, 4, P], U8, "w2s")
+        w2_codes = kept([P, 2, 4, P, 2], U8, "w2_codes")
+        w2_bytes = kept([P, 2, 4, P], U8, "w2_bytes")
         for b in range(2):
-            nc.vector.tensor_copy(w2w[:, b], w2w_raw[b][:].rearrange("p (q t e) -> p t q e", t=4, e=2))
+            on_vector(w2_codes[:, b], w2_words_raw[b][:].rearrange("p (m t e) -> p t m e", t=4, e=2))
 
-        gain_w = kept([P, 2, CH, 4], F32, "gain_w")
-        nc.vector.tensor_copy(gain_w[:], gain_t[:].unsqueeze(2).to_broadcast([P, 2, CH, 4]))
+        gain_wide = kept([P, 2, CHUNK, 4], F32, "gain_wide")
+        on_vector(gain_wide[:], gain_t[:].unsqueeze(2).to_broadcast([P, 2, CHUNK, 4]))
         ident = kept([P, P], F32, "ident")
         make_identity(nc, ident[:])
-        turned = psum.tile([P, 2, P], F32, name="bank", tag="bank")
+        gain_turned = new_bank([P, 2, P])
         for b in range(2):
-            nc.tensor.transpose(turned[:, b, :], gain_w[:, b, 0:32, :].rearrange("p n t -> p (n t)"), ident[:])
+            nc.tensor.transpose(
+                gain_turned[:, b, :], gain_wide[:, b, 0 : P // 4, :].rearrange("p n t -> p (n t)"), ident[:]
+            )
         gain_rows = kept([P, 2, P], F32, "gain_rows")
-        nc.scalar.copy(gain_rows[:], turned[:])
+        on_scalar(gain_rows[:], gain_turned[:])
         gain_bank = psum_keep.tile([P, 2, P], F32, name="gain_bank")
         for b in range(2):
             nc.tensor.transpose(gain_bank[:, b, :], gain_rows[:, b, :], ident[:])
 
         rounded = [
-            [ring.tile([P, 4, P, 4], BF16, name="rounded", align_bytes=64, bufs=4) for a in range(2)] for w in range(3)
+            [ring.tile([P, 4, P, 4], BF16, name="rounded", align_bytes=64, bufs=3) for a in range(2)] for w in range(3)
         ]
-        wq = [[kept([P, PASS], U32, f"wq{w}{a}") for a in range(2)] for w in range(3)]
-        ws = [[kept([P, PASS], U8, f"ws{w}{a}") for a in range(2)] for w in range(3)]
+        w_codes = [[kept([P, PASS], U32, f"w_codes{w}{a}") for a in range(2)] for w in range(3)]
+        w_bytes = [[kept([P, PASS], U8, f"w_bytes{w}{a}") for a in range(2)] for w in range(3)]
 
-        def round_weight(copy, w, a, t0, t1, m0=0, m1=P):
+        def round_weight(copy, w, a, t0, t1):
             copy(
-                rounded[w][a][:, t0:t1, m0:m1, :].rearrange("p t m j -> p m j t"),
-                raw[w][a][:].rearrange("p j (m t) -> p m j t", t=4)[:, m0:m1, :, t0:t1],
+                rounded[w][a][:, t0:t1].rearrange("p t m j -> p m j t"),
+                raw[w][a][:].rearrange("p j (m t) -> p m j t", t=4)[:, :, :, t0:t1],
             )
 
         def quantise_weight(w, a, t0, t1):
             nc.vector.quantize_mx(
-                out=wq[w][a][:, P * t0 : P * t1].bitcast(E4M3),
-                scales=ws[w][a][:, P * t0 : P * t1],
+                out=w_codes[w][a][:, P * t0 : P * t1].bitcast(E4M3),
+                scales=w_bytes[w][a][:, P * t0 : P * t1],
                 in_=rounded[w][a][:, t0:t1].rearrange("p t m j -> p (t m j)"),
             )
 
-        vw = [[kept([P, BANK], U32, f"vw{a}{hf}") for hf in range(2)] for a in range(2)]
+        v_codes = [[kept([P, BANK], U32, f"v_codes{a}{half}") for half in range(2)] for a in range(2)]
 
-        def gather_words(a, hf):
-            nc.vector.tensor_copy(vw[a][hf][:], tabw[a][:].bitcast(U32).indirect(offs_t[:, 32 * hf : 32 * (hf + 1)]))
+        def gather_words(a, half):
+            columns = BANK // PER_COLUMN
+            entries = offs_t[:, columns * half : columns * (half + 1)]
+            on_vector(v_codes[a][half][:], table_words[a][:].bitcast(U32).indirect(entries))
 
         gather_words(0, 0)
         gather_words(0, 1)
-        vs = kept([P, S], U8, "vs")
-        nc.vector.tensor_copy(vs[:], tabs[:].indirect(offs_t[:]))
+        v_bytes = kept([P, S], U8, "v_bytes")
+        on_vector(v_bytes[:], table_scales[:].indirect(offs_t[:]))
         for a in range(2):
-            round_weight(nc.scalar.copy, 0, a, 0, 4)
-            quantise_weight(0, a, 0, 4)
-        nc.vector.tensor_copy(w2s[:], w2s_raw[:].rearrange("p b (q t) -> p b t q", t=4))
+            round_weight(on_scalar, W1_LOW, a, 0, 4)
+            quantise_weight(W1_LOW, a, 0, 4)
+        on_vector(w2_bytes[:], w2_scales_raw[:].rearrange("p b (m t) -> p b t m", t=4))
         gather_words(1, 0)
         gather_words(1, 1)
 
-        hq = [[kept([P, BANK], U32, f"hq{b}{hf}") for hf in range(2)] for b in range(2)]
-        hs = [[kept([P, BANK], U8, f"hs{b}{hf}") for hf in range(2)] for b in range(2)]
+        h_codes = [[kept([P, BANK], U32, f"h_codes{b}{half}") for half in range(2)] for b in range(2)]
+        h_bytes = [[kept([P, BANK], U8, f"h_bytes{b}{half}") for half in range(2)] for b in range(2)]
         g2 = [kept([P, S], F32, f"g2_{t}") for t in range(4)]
 
         def response(b, c):
-            hf, c0 = divmod(CH * c, BANK)
-            bank = psum.tile([P, 4, CH], F32, name="bank", tag="bank")
+            half, c0 = divmod(CHUNK * c, BANK)
+            bank = new_bank([P, 4, CHUNK])
             for a in range(2):
                 for t in range(4):
                     nc.tensor.matmul_mx(
                         out=bank[:, t, :],
-                        lhsT=wq[b][a][:, P * t : P * (t + 1)].bitcast(E4M3),
-                        lhsT_scale=ws[b][a][:, P * t : P * (t + 1)],
-                        rhs=vw[a][hf][:, c0 : c0 + CH].bitcast(E4M3),
-                        rhs_scale=vs[4 * a : P, CH * c : CH * (c + 1)],
+                        lhsT=w_codes[b][a][:, P * t : P * (t + 1)].bitcast(E4M3),
+                        lhsT_scale=w_bytes[b][a][:, P * t : P * (t + 1)],
+                        rhs=v_codes[a][half][:, c0 : c0 + CHUNK].bitcast(E4M3),
+                        rhs_scale=v_bytes[4 * a : P, CHUNK * c : CHUNK * (c + 1)],
                         start=(a, t) == (0, 0),
                         stop=(a, t) == (1, 3),
                     )
-            woven = bank[:].rearrange("p t n -> p n t")
-            sine = ring.tile([P, CH, 4], F32, name="sine", bufs=3)
-            nc.scalar.activation(sine[:], woven, ACT.Sin, scale=0.5)
-            versine = ring.tile([P, CH, 4], F32, name="versine", bufs=4)
+            f = bank[:].rearrange("p t n -> p n t")
+            sine = ring.tile([P, CHUNK, 4], F32, name="sine", bufs=3)
+            nc.scalar.activation(sine[:], f, ACT.Sin, scale=0.5)
+            versine = ring.tile([P, CHUNK, 4], F32, name="versine", bufs=4)
             nc.scalar.activation(versine[:], sine[:], ACT.Square, scale=math.sqrt(2.0))
-            diff = ring.tile([P, CH, 4], F32, name="diff", bufs=4)
-            nc.vector.scalar_tensor_tensor(diff[:], woven, -1.0, versine[:], ALU.add, ALU.add)
+            diff = ring.tile([P, CHUNK, 4], F32, name="diff", bufs=4)
+            nc.vector.scalar_tensor_tensor(diff[:], f, -1.0, versine[:], ALU.add, ALU.add)
             return diff
 
-        def gain_on_gpsimd(dst, diff, b, n0, n1):
-            nc.gpsimd.tensor_tensor(dst[:, n0:n1], diff[:, n0:n1], gain_w[:, b, n0:n1], ALU.mult)
-
-        def gain_on_vector(dst, diff, b, n0, n1):
+        def hidden(b, c):
+            h_round = ring.tile([P, 2, CHUNK, 4], BF16, name="h_round", align_bytes=64)
+            nc.gpsimd.tensor_tensor(h_round[:, 0], response(b, c)[:], gain_wide[:, b], ALU.mult)
             nc.vector.tensor_tensor(
-                dst[:, n0:n1].rearrange("p (r n) t -> p r (n t)", n=32),
-                diff[:, n0:n1].rearrange("p (r n) t -> p r (n t)", n=32),
-                gain_bank[:, b : b + 1, :].to_broadcast([P, (n1 - n0) // 32, P]),
+                h_round[:, 1].rearrange("p (r n) t -> p r (n t)", r=4),
+                response(b, c + 1)[:].rearrange("p (r n) t -> p r (n t)", r=4),
+                gain_bank[:, b : b + 1, :].to_broadcast([P, 4, P]),
                 ALU.mult,
             )
-
-        def hidden(b, c):
-            h_round = ring.tile([P, 2, CH, 4], BF16, name="h_round", align_bytes=64)
-            gain_on_gpsimd(h_round[:, 0], response(b, c), b, 0, CH)
-            diff = response(b, c + 1)
-            gain_on_vector(h_round[:, 1], diff, b, 0, CH)
-            hf, c0 = divmod(CH * c, BANK)
+            half, c0 = divmod(CHUNK * c, BANK)
             nc.vector.quantize_mx(
-                out=hq[b][hf][:, c0 : c0 + 2 * CH].bitcast(E4M3),
-                scales=hs[b][hf][:, c0 : c0 + 2 * CH],
+                out=h_codes[b][half][:, c0 : c0 + 2 * CHUNK].bitcast(E4M3),
+                scales=h_bytes[b][half][:, c0 : c0 + 2 * CHUNK],
                 in_=h_round[:].rearrange("p e n t -> p (e n t)"),
             )
 
-        def skip_size(t, hf):
-            bank = psum.tile([P, BANK], F32, name="bank", tag="bank")
+        def skip_size(t, half):
+            bank = new_bank([P, BANK])
             for a in range(2):
                 nc.tensor.matmul_mx(
                     out=bank[:],
-                    lhsT=wq[2][a][:, P * t : P * (t + 1)].bitcast(E4M3),
-                    lhsT_scale=ws[2][a][:, P * t : P * (t + 1)],
-                    rhs=vw[a][hf][:].bitcast(E4M3),
-                    rhs_scale=vs[4 * a : P, BANK * hf : BANK * (hf + 1)],
+                    lhsT=w_codes[W3][a][:, P * t : P * (t + 1)].bitcast(E4M3),
+                    lhsT_scale=w_bytes[W3][a][:, P * t : P * (t + 1)],
+                    rhs=v_codes[a][half][:].bitcast(E4M3),
+                    rhs_scale=v_bytes[4 * a : P, BANK * half : BANK * (half + 1)],
                     start=(a == 0),
                     stop=(a == 1),
                 )
-            nc.scalar.activation(g2[t][:, BANK * hf : BANK * (hf + 1)], bank[:], ACT.Abs)
+            nc.scalar.activation(g2[t][:, BANK * half : BANK * (half + 1)], bank[:], ACT.Abs)
 
-        def add_features(t, hf, by_gpsimd):
-            bank = psum.tile([P, BANK], F32, name="bank", tag="bank")
+        def second_product(t, half):
+            bank = new_bank([P, BANK])
             for b in range(2):
                 nc.tensor.matmul_mx(
                     out=bank[:],
-                    lhsT=w2w[:, b, t].rearrange("p q e -> p (q e)").bitcast(E2M1),
-                    lhsT_scale=w2s[:, b, t, :],
-                    rhs=hq[b][hf][:].bitcast(E4M3),
-                    rhs_scale=hs[b][hf][:],
+                    lhsT=w2_codes[:, b, t].rearrange("p m e -> p (m e)").bitcast(E2M1),
+                    lhsT_scale=w2_bytes[:, b, t, :],
+                    rhs=h_codes[b][half][:].bitcast(E4M3),
+                    rhs_scale=h_bytes[b][half][:],
                     start=(b == 0),
                     stop=(b == 1),
                 )
-            dst = g2[t][:, BANK * hf : BANK * (hf + 1)]
-            if by_gpsimd:
-                part = ring.tile([P, BANK], F32, name="part")
-                nc.scalar.copy(part[:], bank[:])
-                nc.gpsimd.tensor_tensor(dst, part[:], dst, ALU.add)
-            else:
-                nc.vector.tensor_tensor(dst, bank[:], dst, ALU.add)
+            return bank
 
-        round_weight(nc.vector.tensor_copy, 1, 0, 0, 2)
-        round_weight(nc.vector.tensor_copy, 1, 0, 2, 4)
-        quantise_weight(1, 0, 0, 4)
+        def add_on_vector(t, half):
+            dst = g2[t][:, BANK * half : BANK * (half + 1)]
+            nc.vector.tensor_tensor(dst, second_product(t, half)[:], dst, ALU.add)
+
+        def add_on_gpsimd(t, half):
+            dst = g2[t][:, BANK * half : BANK * (half + 1)]
+            bank = second_product(t, half)
+            part = ring.tile([P, BANK], F32, name="part", bufs=4)
+            on_scalar(part[:], bank[:])
+            nc.gpsimd.tensor_tensor(dst, part[:], dst, ALU.add)
+
+        round_weight(on_vector, W1_HIGH, 0, 0, 4)
+        quantise_weight(W1_HIGH, 0, 0, 4)
         hidden(0, 0)
         hidden(0, 2)
-        round_weight(nc.scalar.copy, 1, 1, 0, 2)
-        round_weight(nc.vector.tensor_copy, 1, 1, 2, 4)
-        quantise_weight(1, 1, 0, 4)
+        round_weight(on_scalar, W1_HIGH, 1, 0, 2)
+        round_weight(on_vector, W1_HIGH, 1, 2, 4)
+        quantise_weight(W1_HIGH, 1, 0, 4)
         hidden(0, 4)
         hidden(0, 6)
-        round_weight(nc.scalar.copy, 2, 0, 0, 2)
-        quantise_weight(2, 0, 0, 2)
-        hidden(1, 0)
-        round_weight(nc.scalar.copy, 2, 1, 0, 2)
-        quantise_weight(2, 1, 0, 2)
-        hidden(1, 2)
+        for a in range(2):
+            round_weight(on_scalar, W3, a, 0, 2)
+            quantise_weight(W3, a, 0, 2)
+            hidden(1, 2 * a)
         hidden(1, 4)
         skip_size(0, 0)
-        add_features(0, 0, False)
+        add_on_vector(0, 0)
         hidden(1, 6)
         skip_size(0, 1)
         skip_size(1, 0)
-        add_features(1, 0, False)
-        add_features(0, 1, False)
+        add_on_vector(1, 0)
+        add_on_vector(0, 1)
         skip_size(1, 1)
         for a in range(2):
-            round_weight(nc.scalar.copy, 2, a, 2, 4)
-            quantise_weight(2, a, 2, 4)
+            round_weight(on_scalar, W3, a, 2, 4)
+            quantise_weight(W3, a, 2, 4)
 
         y = kept([P, 4, M], F32, "y")
-        yq = kept([P, M], U32, "yq")
-        ys = kept([P, M], U8, "ys")
+        y_codes = kept([P, M], U32, "y_codes")
+        y_bytes = kept([P, M], U8, "y_bytes")
         out0_rows = out_0.rearrange("(p t) m -> p t m", t=4)
         out1_words = out_1[0].rearrange("p m t -> p (m t)").bitcast(I32)
 
+        def larger_feature(t):
+            left = ring.tile([P, M], F32, name="left")
+            right = ring.tile([P, M], F32, name="right")
+            larger = ring.tile([P, M], F32, name="larger")
+            on_vector(left[:], g2[t][:].indirect(pos1_t[:]))
+            on_vector(right[:], g2[t][:].indirect(pos2_t[:]))
+            nc.vector.tensor_tensor(larger[:], left[:], right[:], ALU.max)
+            return larger
+
         def turned_copy(src, name, scale):
-            bank = psum.tile([P, 4, P], F32, name="bank", tag="bank")
+            bank = new_bank([P, 4, P])
             for i in range(4):
                 nc.tensor.transpose(bank[:, i, :], src[:, P * i : P * (i + 1)], ident[:])
             dst = ring.tile([P, 4, P], F32, name=name)
@@ -266,48 +278,39 @@ def tile_list_scaffold_lashing_features_kernel(
             return dst
 
         def subtract_on_tensor(t, larger):
-            base_turned = turned_copy(base_t[:, t, :], "base_turned", -1.0)
-            larger_turned = turned_copy(larger, "larger_turned", 1.0)
-            bank = psum.tile([P, 4, P], F32, name="bank", tag="bank")
+            terms = [turned_copy(base_t[:, t, :], "base_turned", -1.0), turned_copy(larger[:], "larger_turned", 1.0)]
+            bank = new_bank([P, 4, P])
             for i in range(4):
-                nc.tensor.matmul(bank[:, i, :], base_turned[:, i, :], ident[:], start=True, stop=False, is_transpose=True)
-                nc.tensor.matmul(bank[:, i, :], larger_turned[:, i, :], ident[:], start=False, stop=True, is_transpose=True)
-            nc.scalar.copy(y[:, t, :], bank[:].rearrange("p i m -> p (i m)"))
+                for e in range(2):
+                    nc.tensor.matmul(
+                        bank[:, i, :], terms[e][:, i, :], ident[:], start=(e == 0), stop=(e == 1), is_transpose=True
+                    )
+            on_scalar(y[:, t, :], bank[:].rearrange("p i m -> p (i m)"))
 
-        def joints(t, m0, m1, engine):
-            left = ring.tile([P, m1 - m0], F32, name="left")
-            right = ring.tile([P, m1 - m0], F32, name="right")
-            larger = ring.tile([P, m1 - m0], F32, name="larger")
-            nc.vector.tensor_copy(left[:], g2[t][:].indirect(pos1_t[:, m0 // 16 : m1 // 16]))
-            nc.vector.tensor_copy(right[:], g2[t][:].indirect(pos2_t[:, m0 // 16 : m1 // 16]))
-            nc.vector.tensor_tensor(larger[:], left[:], right[:], ALU.max)
-            if engine is None:
-                subtract_on_tensor(t, larger[:])
-            else:
-                engine.tensor_tensor(y[:, t, m0:m1], larger[:], base_t[:, t, m0:m1], ALU.subtract)
-            nc.sync.dma_start(out0_rows[:, t, m0:m1], y[:, t, m0:m1])
-
-        def planes(copy, m0, m1):
+        def quantise_result(copy, m0, m1):
             y_round = ring.tile([P, m1 - m0, 4], BF16, name="y_round", align_bytes=64)
             copy(
                 y_round[:].rearrange("p (c i) t -> p c t i", i=4), y[:, :, m0:m1].rearrange("p t (c i) -> p c t i", i=4)
             )
             nc.vector.quantize_mx(
-                out=yq[:, m0:m1].bitcast(E4M3), scales=ys[:, m0:m1], in_=y_round[:].rearrange("p m t -> p (m t)")
+                out=y_codes[:, m0:m1].bitcast(E4M3),
+                scales=y_bytes[:, m0:m1],
+                in_=y_round[:].rearrange("p m t -> p (m t)"),
             )
-            nc.scalar.dma_start(out1_words[:, m0:m1], yq[:, m0:m1].bitcast(I32))
+            nc.scalar.dma_start(out1_words[:, m0:m1], y_codes[:, m0:m1].bitcast(I32))
 
-        add_features(1, 1, False)
+        add_on_gpsimd(1, 1)
         for t in range(3):
-            if t < 2:
-                for hf in range(2):
-                    skip_size(t + 2, hf)
-                    add_features(t + 2, hf, False)
-            joints(t, 0, M, None)
-        joints(3, 0, M // 2, nc.vector)
-        joints(3, M // 2, M, nc.vector)
-        planes(nc.scalar.copy, 0, M // 2)
-        planes(nc.vector.tensor_copy, M // 2, M)
+            if t + 2 < 4:
+                for half in range(2):
+                    skip_size(t + 2, half)
+                    add_on_gpsimd(t + 2, half)
+            subtract_on_tensor(t, larger_feature(t))
+            nc.sync.dma_start(out0_rows[:, t, :], y[:, t, :])
+        nc.vector.tensor_tensor(y[:, 3, :], larger_feature(3)[:], base_t[:, 3, :], ALU.subtract)
+        nc.sync.dma_start(out0_rows[:, 3, :], y[:, 3, :])
+        quantise_result(on_vector, 0, M // 2)
+        quantise_result(on_scalar, M // 2, M)
         for q in range(4):
             queue = nc.sync if q % 2 == 0 else nc.scalar
-            queue.dma_start(out_2[0, 4 * q : 4 * q + 4, :].bitcast(I32), ys[32 * q : 32 * q + 4, :].bitcast(I32))
+            queue.dma_start(out_2[0, 4 * q : 4 * q + 4, :].bitcast(I32), y_bytes[32 * q : 32 * q + 4, :].bitcast(I32))

import math
from contextlib import ExitStack

import concourse.mybir as mybir
from concourse.masks import make_identity

K, T, S, H, N, M = 1024, 4096, 1024, 1024, 512, 512
FLOPS = 2 * K * H * S + 2 * K * N * S + 2 * H * N * S

F32 = mybir.dt.float32
BF16 = mybir.dt.bfloat16
I32 = mybir.dt.int32
U32 = mybir.dt.uint32
U16 = mybir.dt.uint16
U8 = mybir.dt.uint8
E4M3 = mybir.dt.float8_e4m3fn_x4
E2M1 = mybir.dt.float4_e2m1fn_x4
ACT = mybir.ActivationFunctionType
ALU = mybir.AluOpType

P = 128
PASS = 512
BANK = 512
CHUNK = 128
PER_COLUMN = 16
QUADRANTS = (0, 2, 1, 3)
W1_LOW, W1_HIGH, W3 = 0, 1, 2


def tile_list_scaffold_lashing_features_kernel(
    tc, tab_words, tab_scales, offs, pos1, pos2, w1, gain, w2_words, w2_scales, w3, base, out_0, out_1, out_2
):
    nc = tc.nc
    on_vector, on_scalar = nc.vector.tensor_copy, nc.scalar.copy
    with ExitStack() as ctx:
        keep = ctx.enter_context(tc.tile_pool(name="keep", bufs=1))
        ring = ctx.enter_context(tc.tile_pool(name="ring", bufs=2))
        psum = ctx.enter_context(tc.psum_pool(name="psum", bufs=7))
        psum_keep = ctx.enter_context(tc.psum_pool(name="psum_keep", bufs=1))

        def kept(shape, dtype, name):
            return keep.tile(shape, dtype, name=name, align_bytes=64)

        def new_bank(shape):
            return psum.tile(shape, F32, name="bank", tag="bank")

        offs_t = keep.tile([P, S // PER_COLUMN], U16, name="offs_t")
        pos1_t = keep.tile([P, M // PER_COLUMN], U16, name="pos1_t")
        pos2_t = keep.tile([P, M // PER_COLUMN], U16, name="pos2_t")
        table_words = [kept([P, T], I32, f"table_words{a}") for a in range(2)]
        table_scales = kept([P, T], U8, "table_scales")
        w2_words_raw = [kept([P, 2 * N], U8, f"w2_words_raw{b}") for b in range(2)]
        w2_scales_raw = kept([P, 2, N], U8, "w2_scales_raw")
        gain_t = kept([P, 2, 4], F32, "gain_t")
        base_t = kept([P, 4, M], F32, "base_t")
        weights = [w1[:, 0:PASS], w1[:, PASS : 2 * PASS], w3]
        raw = [[kept([P, 4, PASS], F32, f"raw{w}{a}") for a in range(2)] for w in range(3)]

        nc.vector.memset(table_scales[:].bitcast(I32), 0)
        nc.gpsimd.memset(w2_scales_raw[:].rearrange("p b c -> p (b c)").bitcast(I32), 0)

        def load_weight(w, a):
            rows = weights[w][PASS * a : PASS * (a + 1), :]
            nc.sync.dma_start(raw[w][a][:], rows.rearrange("(p j) c -> p j c", j=4))

        words = [tab_words[a].rearrange("p t i -> p (t i)").bitcast(I32) for a in range(2)]
        nc.sync.dma_start(table_words[0][:, 0 : T // 2], words[0][:, 0 : T // 2])
        nc.sync.dma_start(offs_t[:], offs)
        nc.sync.dma_start(pos1_t[:], pos1)
        nc.sync.dma_start(pos2_t[:], pos2)
        nc.sync.dma_start(gain_t[:], gain.rearrange("(b p t) -> p b t", b=2, t=4))
        for b in range(2):
            nc.sync.dma_start(w2_words_raw[b][:].bitcast(I32), w2_words[b].bitcast(I32))
        nc.sync.dma_start(table_words[0][:, T // 2 : T], words[0][:, T // 2 : T])
        for q in QUADRANTS:
            nc.sync.dma_start(
                table_scales[32 * q : 32 * q + 8, :].bitcast(I32), tab_scales[:, 4 * q : 4 * q + 4, :].bitcast(I32)
            )
        for a in range(2):
            load_weight(W1_LOW, a)
        for q in QUADRANTS:
            nc.sync.dma_start(
                w2_scales_raw[32 * q : 32 * q + 4, :, :].bitcast(I32),
                w2_scales[:, 4 * q : 4 * q + 4, :].rearrange("b r c -> r b c").bitcast(I32),
            )
        nc.sync.dma_start(table_words[1][:], words[1])
        for w in (W1_HIGH, W3):
            for a in range(2):
                load_weight(w, a)
        nc.sync.dma_start(base_t[:], base.rearrange("(p t) m -> p t m", t=4))

        w2_codes = kept([P, 2, 4, P, 2], U8, "w2_codes")
        w2_bytes = kept([P, 2, 4, P], U8, "w2_bytes")
        for b in range(2):
            on_vector(w2_codes[:, b], w2_words_raw[b][:].rearrange("p (m t e) -> p t m e", t=4, e=2))

        gain_wide = kept([P, 2, CHUNK, 4], F32, "gain_wide")
        on_vector(gain_wide[:], gain_t[:].unsqueeze(2).to_broadcast([P, 2, CHUNK, 4]))
        ident = kept([P, P], F32, "ident")
        make_identity(nc, ident[:])
        gain_turned = new_bank([P, 2, P])
        for b in range(2):
            nc.tensor.transpose(
                gain_turned[:, b, :], gain_wide[:, b, 0 : P // 4, :].rearrange("p n t -> p (n t)"), ident[:]
            )
        gain_rows = kept([P, 2, P], F32, "gain_rows")
        on_scalar(gain_rows[:], gain_turned[:])
        gain_bank = psum_keep.tile([P, 2, P], F32, name="gain_bank")
        for b in range(2):
            nc.tensor.transpose(gain_bank[:, b, :], gain_rows[:, b, :], ident[:])

        rounded = [
            [ring.tile([P, 4, P, 4], BF16, name="rounded", align_bytes=64, bufs=3) for a in range(2)] for w in range(3)
        ]
        w_codes = [[kept([P, PASS], U32, f"w_codes{w}{a}") for a in range(2)] for w in range(3)]
        w_bytes = [[kept([P, PASS], U8, f"w_bytes{w}{a}") for a in range(2)] for w in range(3)]

        def round_weight(copy, w, a, t0, t1):
            copy(
                rounded[w][a][:, t0:t1].rearrange("p t m j -> p m j t"),
                raw[w][a][:].rearrange("p j (m t) -> p m j t", t=4)[:, :, :, t0:t1],
            )

        def quantise_weight(w, a, t0, t1):
            nc.vector.quantize_mx(
                out=w_codes[w][a][:, P * t0 : P * t1].bitcast(E4M3),
                scales=w_bytes[w][a][:, P * t0 : P * t1],
                in_=rounded[w][a][:, t0:t1].rearrange("p t m j -> p (t m j)"),
            )

        v_codes = [[kept([P, BANK], U32, f"v_codes{a}{half}") for half in range(2)] for a in range(2)]

        def gather_words(a, half):
            columns = BANK // PER_COLUMN
            entries = offs_t[:, columns * half : columns * (half + 1)]
            on_vector(v_codes[a][half][:], table_words[a][:].bitcast(U32).indirect(entries))

        gather_words(0, 0)
        gather_words(0, 1)
        v_bytes = kept([P, S], U8, "v_bytes")
        on_vector(v_bytes[:], table_scales[:].indirect(offs_t[:]))
        for a in range(2):
            round_weight(on_scalar, W1_LOW, a, 0, 4)
            quantise_weight(W1_LOW, a, 0, 4)
        on_vector(w2_bytes[:], w2_scales_raw[:].rearrange("p b (m t) -> p b t m", t=4))
        gather_words(1, 0)
        gather_words(1, 1)

        h_codes = [[kept([P, BANK], U32, f"h_codes{b}{half}") for half in range(2)] for b in range(2)]
        h_bytes = [[kept([P, BANK], U8, f"h_bytes{b}{half}") for half in range(2)] for b in range(2)]
        g2 = [kept([P, S], F32, f"g2_{t}") for t in range(4)]

        def response(b, c):
            half, c0 = divmod(CHUNK * c, BANK)
            bank = new_bank([P, 4, CHUNK])
            for a in range(2):
                for t in range(4):
                    nc.tensor.matmul_mx(
                        out=bank[:, t, :],
                        lhsT=w_codes[b][a][:, P * t : P * (t + 1)].bitcast(E4M3),
                        lhsT_scale=w_bytes[b][a][:, P * t : P * (t + 1)],
                        rhs=v_codes[a][half][:, c0 : c0 + CHUNK].bitcast(E4M3),
                        rhs_scale=v_bytes[4 * a : P, CHUNK * c : CHUNK * (c + 1)],
                        start=(a, t) == (0, 0),
                        stop=(a, t) == (1, 3),
                    )
            f = bank[:].rearrange("p t n -> p n t")
            sine = ring.tile([P, CHUNK, 4], F32, name="sine", bufs=3)
            nc.scalar.activation(sine[:], f, ACT.Sin, scale=0.5)
            versine = ring.tile([P, CHUNK, 4], F32, name="versine", bufs=4)
            nc.scalar.activation(versine[:], sine[:], ACT.Square, scale=math.sqrt(2.0))
            diff = ring.tile([P, CHUNK, 4], F32, name="diff", bufs=4)
            nc.vector.scalar_tensor_tensor(diff[:], f, -1.0, versine[:], ALU.add, ALU.add)
            return diff

        def hidden(b, c):
            h_round = ring.tile([P, 2, CHUNK, 4], BF16, name="h_round", align_bytes=64)
            nc.gpsimd.tensor_tensor(h_round[:, 0], response(b, c)[:], gain_wide[:, b], ALU.mult)
            nc.vector.tensor_tensor(
                h_round[:, 1].rearrange("p (r n) t -> p r (n t)", r=4),
                response(b, c + 1)[:].rearrange("p (r n) t -> p r (n t)", r=4),
                gain_bank[:, b : b + 1, :].to_broadcast([P, 4, P]),
                ALU.mult,
            )
            half, c0 = divmod(CHUNK * c, BANK)
            nc.vector.quantize_mx(
                out=h_codes[b][half][:, c0 : c0 + 2 * CHUNK].bitcast(E4M3),
                scales=h_bytes[b][half][:, c0 : c0 + 2 * CHUNK],
                in_=h_round[:].rearrange("p e n t -> p (e n t)"),
            )

        def skip_size(t, half):
            bank = new_bank([P, BANK])
            for a in range(2):
                nc.tensor.matmul_mx(
                    out=bank[:],
                    lhsT=w_codes[W3][a][:, P * t : P * (t + 1)].bitcast(E4M3),
                    lhsT_scale=w_bytes[W3][a][:, P * t : P * (t + 1)],
                    rhs=v_codes[a][half][:].bitcast(E4M3),
                    rhs_scale=v_bytes[4 * a : P, BANK * half : BANK * (half + 1)],
                    start=(a == 0),
                    stop=(a == 1),
                )
            nc.scalar.activation(g2[t][:, BANK * half : BANK * (half + 1)], bank[:], ACT.Abs)

        def second_product(t, half):
            bank = new_bank([P, BANK])
            for b in range(2):
                nc.tensor.matmul_mx(
                    out=bank[:],
                    lhsT=w2_codes[:, b, t].rearrange("p m e -> p (m e)").bitcast(E2M1),
                    lhsT_scale=w2_bytes[:, b, t, :],
                    rhs=h_codes[b][half][:].bitcast(E4M3),
                    rhs_scale=h_bytes[b][half][:],
                    start=(b == 0),
                    stop=(b == 1),
                )
            return bank

        def add_on_vector(t, half):
            dst = g2[t][:, BANK * half : BANK * (half + 1)]
            nc.vector.tensor_tensor(dst, second_product(t, half)[:], dst, ALU.add)

        def add_on_gpsimd(t, half):
            dst = g2[t][:, BANK * half : BANK * (half + 1)]
            bank = second_product(t, half)
            part = ring.tile([P, BANK], F32, name="part", bufs=4)
            on_scalar(part[:], bank[:])
            nc.gpsimd.tensor_tensor(dst, part[:], dst, ALU.add)

        round_weight(on_vector, W1_HIGH, 0, 0, 4)
        quantise_weight(W1_HIGH, 0, 0, 4)
        hidden(0, 0)
        hidden(0, 2)
        round_weight(on_scalar, W1_HIGH, 1, 0, 2)
        round_weight(on_vector, W1_HIGH, 1, 2, 4)
        quantise_weight(W1_HIGH, 1, 0, 4)
        hidden(0, 4)
        hidden(0, 6)
        for a in range(2):
            round_weight(on_scalar, W3, a, 0, 2)
            quantise_weight(W3, a, 0, 2)
            hidden(1, 2 * a)
        hidden(1, 4)
        skip_size(0, 0)
        add_on_vector(0, 0)
        hidden(1, 6)
        skip_size(0, 1)
        skip_size(1, 0)
        add_on_vector(1, 0)
        add_on_vector(0, 1)
        skip_size(1, 1)
        for a in range(2):
            round_weight(on_scalar, W3, a, 2, 4)
            quantise_weight(W3, a, 2, 4)

        y = kept([P, 4, M], F32, "y")
        y_codes = kept([P, M], U32, "y_codes")
        y_bytes = kept([P, M], U8, "y_bytes")
        out0_rows = out_0.rearrange("(p t) m -> p t m", t=4)
        out1_words = out_1[0].rearrange("p m t -> p (m t)").bitcast(I32)

        def larger_feature(t):
            left = ring.tile([P, M], F32, name="left")
            right = ring.tile([P, M], F32, name="right")
            larger = ring.tile([P, M], F32, name="larger")
            on_vector(left[:], g2[t][:].indirect(pos1_t[:]))
            on_vector(right[:], g2[t][:].indirect(pos2_t[:]))
            nc.vector.tensor_tensor(larger[:], left[:], right[:], ALU.max)
            return larger

        def turned_copy(src, name, scale):
            bank = new_bank([P, 4, P])
            for i in range(4):
                nc.tensor.transpose(bank[:, i, :], src[:, P * i : P * (i + 1)], ident[:])
            dst = ring.tile([P, 4, P], F32, name=name)
            nc.scalar.activation(dst[:], bank[:], ACT.Copy, scale=scale)
            return dst

        def subtract_on_tensor(t, larger):
            terms = [turned_copy(base_t[:, t, :], "base_turned", -1.0), turned_copy(larger[:], "larger_turned", 1.0)]
            bank = new_bank([P, 4, P])
            for i in range(4):
                for e in range(2):
                    nc.tensor.matmul(
                        bank[:, i, :], terms[e][:, i, :], ident[:], start=(e == 0), stop=(e == 1), is_transpose=True
                    )
            on_scalar(y[:, t, :], bank[:].rearrange("p i m -> p (i m)"))

        def quantise_result(copy, m0, m1):
            y_round = ring.tile([P, m1 - m0, 4], BF16, name="y_round", align_bytes=64)
            copy(
                y_round[:].rearrange("p (c i) t -> p c t i", i=4), y[:, :, m0:m1].rearrange("p t (c i) -> p c t i", i=4)
            )
            nc.vector.quantize_mx(
                out=y_codes[:, m0:m1].bitcast(E4M3),
                scales=y_bytes[:, m0:m1],
                in_=y_round[:].rearrange("p m t -> p (m t)"),
            )
            nc.scalar.dma_start(out1_words[:, m0:m1], y_codes[:, m0:m1].bitcast(I32))

        add_on_gpsimd(1, 1)
        for t in range(3):
            if t + 2 < 4:
                for half in range(2):
                    skip_size(t + 2, half)
                    add_on_gpsimd(t + 2, half)
            subtract_on_tensor(t, larger_feature(t))
            nc.sync.dma_start(out0_rows[:, t, :], y[:, t, :])
        nc.vector.tensor_tensor(y[:, 3, :], larger_feature(3)[:], base_t[:, 3, :], ALU.subtract)
        nc.sync.dma_start(out0_rows[:, 3, :], y[:, 3, :])
        quantise_result(on_vector, 0, M // 2)
        quantise_result(on_scalar, M // 2, M)
        for q in range(4):
            queue = nc.sync if q % 2 == 0 else nc.scalar
            queue.dma_start(out_2[0, 4 * q : 4 * q + 4, :].bitcast(I32), y_bytes[32 * q : 32 * q + 4, :].bitcast(I32))
